import numpy as np
import ml_dtypes


def mxq(x, axis, fmt="e4m3"):
    dtype, down = {"e4m3": (ml_dtypes.float8_e4m3fn, 7), "e5m2": (ml_dtypes.float8_e5m2, 14)}[fmt]
    v = np.moveaxis(np.asarray(x, np.float32).astype(ml_dtypes.bfloat16).astype(np.float64), axis, -1)
    blocks = v.reshape(v.shape[:-1] + (-1, 32))
    amax = np.abs(blocks).max(-1, keepdims=True)
    byte = np.maximum(np.where(amax > 0, np.frexp(amax)[1] - 1 + 127, 0) - down, 1)
    scale = np.exp2(byte - 127.0)
    codes = (blocks / scale).astype(np.float32).astype(dtype).astype(np.float64)
    return np.moveaxis((codes * scale).reshape(v.shape), -1, axis)


WIDE = False


def mx_kscale(k):
    if not WIDE:
        return np.ones(k)
    levels = np.array([24, -24, 12, -12, 0])
    if k % 512:
        return np.exp2(np.random.permutation(np.resize(levels, k // 32))).repeat(32)
    a = np.empty((k // 512, 16))
    for p in range(k // 512):
        a[p, :8] = np.random.permutation(np.resize(levels, 8))
        for g in range(8):
            far = levels[np.abs(levels - a[p, g]) >= 10]
            a[p, g + 8] = far[np.random.randint(len(far))]
    return np.exp2(a.ravel()).repeat(32)


def f64(x):
    return np.asarray(x).astype(np.float64)


def striped(idx):
    return np.tile(idx.reshape(-1, 16).T, (8, 1)).astype(np.uint16)


def unstriped(offs):
    return offs[:16].T.reshape(-1).astype(np.int64)


E2M1 = np.array([0.0, 0.5, 1.0, 1.5, 2.0, 3.0, 4.0, 6.0, -0.0, -0.5, -1.0, -1.5, -2.0, -3.0, -4.0, -6.0])


def pack_weight(w, fmt):
    k, n = w.shape
    w = f64(np.asarray(w, np.float32).astype(ml_dtypes.bfloat16)).reshape(k // 32, 32, n)
    amax = np.abs(w).max(1)
    if fmt == "e4m3":
        byte = np.frexp(amax)[1] - 1 + 127 - 7
    else:
        mant, ex = np.frexp(amax / 6.0)
        byte = np.where(mant > 0.5, ex, ex - 1) + 127
    byte = np.clip(np.where(amax > 0, byte, 1), 1, 254)
    scaled = (w * np.exp2(127.0 - byte)[:, None, :]).reshape(k, n).astype(np.float32)
    by_word = np.ascontiguousarray(scaled.reshape(k // 512, 128, 4, n).transpose(0, 1, 3, 2))
    if fmt == "e4m3":
        words = by_word.astype(ml_dtypes.float8_e4m3fn).view(np.uint8)
    else:
        c = by_word.astype(ml_dtypes.float4_e2m1fn).view(np.uint8) & 0xF
        words = (c[..., 0::2] | (c[..., 1::2] << 4)).reshape(k // 512, 128, 2 * n)
    return np.ascontiguousarray(words), np.ascontiguousarray(byte.astype(np.uint8).reshape(k // 512, 16, n))


def unpack_weight(words, scales, fmt):
    g, _, n = scales.shape
    words = np.ascontiguousarray(words).reshape(g, 128, n, -1)
    if fmt == "e4m3":
        vals = words.view(ml_dtypes.float8_e4m3fn).astype(np.float64)
    else:
        nib = np.empty((g, 128, n, 4), np.uint8)
        nib[..., 0::2] = words & 0xF
        nib[..., 1::2] = words >> 4
        vals = E2M1[nib]
    vals = vals * np.repeat(np.exp2(scales.astype(np.float64) - 127.0), 8, axis=1)[..., None]
    return vals.transpose(0, 1, 3, 2).reshape(g * 512, n)


def sigm(f):
    return 1.0 / (1.0 + np.exp(-np.maximum(f, -700.0)))


K, N, T, J = 1024, 256, 1024, 512


def setup_inputs():
    n = np.random.standard_normal
    s = mx_kscale(K)[:, None]
    wh = n((K, N)) / np.sqrt(K) / s
    p_tab = pack_weight(n((K, T)) * s, "e4m3")
    p_wg = pack_weight(n((K, N)) / np.sqrt(K) / s, "e4m3")
    p_wh4 = pack_weight(wh[512:], "e2m1")
    return {
        "tab_words": p_tab[0],
        "tab_scales": p_tab[1],
        "wg_words": p_wg[0],
        "wg_scales": p_wg[1],
        "wh8": (wh[:512]).astype(np.float32),
        "wh4_words": p_wh4[0],
        "wh4_scales": p_wh4[1],
        "bg": (0.3 * n(N) - 1.0).astype(np.float32),
        "rT": (n((N, T))).astype(np.float32),
        "offs": striped(np.random.permutation(T)[:J]),
    }


def reference(tab_words, tab_scales, wg_words, wg_scales, wh8, wh4_words, wh4_scales, bg, rT, offs):
    idx = unstriped(offs)
    tab_ = unpack_weight(tab_words, tab_scales, "e4m3")[:, idx]
    wg_ = unpack_weight(wg_words, wg_scales, "e4m3")
    wh8_ = mxq(f64(wh8), 0, "e4m3")
    wh4_ = unpack_weight(wh4_words, wh4_scales, "e2m1")
    ga = wg_.T @ tab_
    gate = sigm(ga + f64(bg)[:, None])
    ha = wh8_.T @ tab_[:512] + wh4_.T @ tab_[512:]
    return f64(rT)[:, idx] + gate * (np.tanh(ha) - f64(rT)[:, idx])

@@ -1,0 +1,186 @@
+from contextlib import ExitStack
+
+import concourse.mybir as mybir
+
+K, N, T, J = 1024, 256, 1024, 512
+FLOPS = 2 * 2 * K * N * J
+
+F32 = mybir.dt.float32
+BF16 = mybir.dt.bfloat16
+I32 = mybir.dt.int32
+U32 = mybir.dt.uint32
+U16 = mybir.dt.uint16
+U8 = mybir.dt.uint8
+FP8X4 = mybir.dt.float8_e4m3fn_x4
+FP4X4 = mybir.dt.float4_e2m1fn_x4
+ACT = mybir.ActivationFunctionType
+ALU = mybir.AluOpType
+
+P = 128
+PACK = 4
+QUADS = 4
+PASSES = 2
+HALVES = N // P
+CHUNK = 256
+TAB_ROW0 = (4, 0)
+
+
+def tile_list_hwayt_qf_tanh_kernel(
+    tc, tab_words, tab_scales, wg_words, wg_scales, wh8, wh4_words, wh4_scales, bg, rT, offs, out
+):
+    nc = tc.nc
+    with ExitStack() as ctx:
+        sb = ctx.enter_context(tc.tile_pool(name="sb", bufs=1))
+        ps = ctx.enter_context(tc.psum_pool(name="ps", bufs=1))
+
+        held = ctx.enter_context(tc.tile_pool(name="held", bufs=1))
+        offsets = held.tile([P, J // 16], U16, name="offsets")
+        tab_w0 = sb.tile([P, T], U32, name="tab_w0", align_bytes=64)
+        tab_w1 = sb.tile([P, T], U32, name="tab_w1", align_bytes=64)
+        tab_w = [tab_w0, tab_w1]
+        tab_s = sb.tile([P, T], U8, name="tab_s", align_bytes=64)
+        wg_s = sb.tile([P, PASSES, N], U8, name="wg_s", align_bytes=64)
+        wh4_w = sb.tile([P, 2 * N], U8, name="wh4_w", align_bytes=64)
+        wh4_s = sb.tile([P, N], U8, name="wh4_s", align_bytes=64)
+        wh8_raw = sb.tile([P, PACK, N], F32, name="wh8_raw", align_bytes=64)
+        bias = sb.tile([P, HALVES], F32, name="bias")
+        half_bias = sb.tile([P, HALVES], F32, name="half_bias")
+        got_s = sb.tile([P, J], U8, name="got_s", align_bytes=64)
+
+        nc.gpsimd.memset(wh4_s[:].bitcast(I32), 0)
+        nc.vector.memset(wg_s[:].bitcast(I32), 0)
+        nc.vector.memset(tab_s[:].bitcast(I32)[32:64, :], 0)
+        nc.vector.memset(tab_s[:].bitcast(I32)[64:128, :], 0)
+        nc.vector.memset(got_s[:].bitcast(I32), 0)
+
+        def load_wg_scales(engine, q):
+            engine.dma_start(
+                wg_s[:].bitcast(I32)[32 * q : 32 * q + 4, :, :],
+                wg_scales[:, 4 * q : 4 * q + 4, :].rearrange("a r n -> r a n").bitcast(I32),
+            )
+
+        def load_wh4_scales(engine, q):
+            engine.dma_start(
+                wh4_s[:].bitcast(I32)[32 * q : 32 * q + 4, :], wh4_scales[0, 4 * q : 4 * q + 4, :].bitcast(I32)
+            )
+
+        nc.sync.dma_start(offsets[:], offs)
+        for a, engine in enumerate((nc.sync, nc.scalar)):
+            first = 16 * (1 - a)
+            engine.dma_start(
+                tab_s[:].bitcast(I32)[first : first + 16, :],
+                tab_scales[a].bitcast(I32).rearrange("(q r) t -> r q t", r=4),
+            )
+        def load_words(a):
+            nc.sync.dma_start(tab_w[a][:].bitcast(I32), tab_words[a].rearrange("p t i -> p (t i)").bitcast(I32))
+
+        load_words(0)
+        nc.sync.dma_start(wh8_raw[:], wh8.rearrange("(p i) n -> p i n", i=PACK))
+        nc.scalar.dma_start(wh4_w[:].bitcast(I32), wh4_words[0].bitcast(I32))
+        for q, engine in enumerate((nc.scalar, nc.scalar, nc.sync, nc.gpsimd)):
+            load_wh4_scales(engine, q)
+        load_words(1)
+
+        got_w = [sb.tile([P, J], U32, name=f"got_w{a}", align_bytes=64) for a in range(PASSES)]
+        got_rows = sb.tile([P, J], U8, name="got_rows", align_bytes=64)
+        nc.vector.tensor_copy(got_rows[:], tab_s[:].indirect(offsets[:]))
+        carry0 = sb.tile([P, T], F32, name="carry0", align_bytes=64)
+        carry1 = sb.tile([P, T], F32, name="carry1", align_bytes=64)
+        for q in range(QUADS):
+            nc.sync.dma_start(
+                got_s[:].bitcast(I32)[32 * q : 32 * q + 8, :], got_rows[:].bitcast(I32)[q:32:4, :]
+            )
+        nc.sync.dma_start(carry0[:], rT[0:P, :])
+        nc.sync.dma_start(carry1[:], rT[P : 2 * P, :])
+        nc.vector.tensor_copy(got_w[0][:], tab_w[0][:].indirect(offsets[:]))
+        wg_w = sb.tile([P, PASSES, N], U32, name="wg_w", align_bytes=64)
+        nc.sync.dma_start(wg_w[:].bitcast(I32), wg_words.rearrange("a p n i -> p a (n i)").bitcast(I32))
+        for q in range(QUADS):
+            load_wg_scales(nc.sync, q)
+        with nc.allow_non_contiguous_dma(reason="one bias value for each partition and half"):
+            nc.sync.dma_start(bias[:], bg.rearrange("(m p) -> p m", p=P))
+        nc.scalar.mul(half_bias[:], bias[:], 0.5)
+        carry = [carry0[:], carry1[:]]
+
+        wh8_w, wh8_s = [], []
+        for m in range(HALVES):
+            grouped = sb.tile([P, P, PACK], BF16, name=f"grouped{m}", tag=f"half{m}", align_bytes=64)
+            nc.scalar.activation(
+                grouped[:].rearrange("p (c e) i -> p c i e", e=4),
+                wh8_raw[:, :, m * P : (m + 1) * P].rearrange("p i (c e) -> p c i e", e=4),
+                ACT.Copy,
+            )
+            words = sb.tile([P, P], U32, name=f"wh8_w{m}", align_bytes=64)
+            scales = sb.tile([P, P], U8, name=f"wh8_s{m}", align_bytes=64)
+            nc.vector.quantize_mx(
+                out=words[:].bitcast(FP8X4), scales=scales[:], in_=grouped[:].rearrange("p c i -> p (c i)")
+            )
+            wh8_w.append(words)
+            wh8_s.append(scales)
+            if m == 0:
+                nc.vector.tensor_copy(got_w[1][:], tab_w[1][:].indirect(offsets[:]))
+
+        picked = [sb.tile([P, J], F32, name=f"picked{m}", tag=f"half{m}", align_bytes=64) for m in range(HALVES)]
+        for m in range(HALVES):
+            nc.vector.tensor_copy(picked[m][:], carry[m].indirect(offsets[:]))
+
+        def table(a):
+            return dict(rhs=got_w[a][:].bitcast(FP8X4), rhs_scale=got_s[TAB_ROW0[a] : P, :])
+
+        ha = [ps.tile([P, J], F32, name=f"ha{m}") for m in range(HALVES)]
+        ga = [ps.tile([P, J], F32, name=f"ga{m}") for m in range(HALVES)]
+        made = [sb.tile([P, J], F32, name=f"made{m}") for m in range(HALVES)]
+        swing = [sb.tile([P, J], F32, name=f"swing{m}") for m in range(HALVES)]
+        diff = [sb.tile([P, J], F32, name=f"diff{m}") for m in range(HALVES)]
+        step = [sb.tile([P, J], F32, name=f"step{m}") for m in range(HALVES)]
+        result = [sb.tile([P, J], F32, name=f"result{m}") for m in range(HALVES)]
+        cols = [slice(m * P, (m + 1) * P) for m in range(HALVES)]
+        for m in range(HALVES):
+            nc.tensor.matmul_mx(
+                out=ha[m][:],
+                lhsT=wh8_w[m][:].bitcast(FP8X4),
+                lhsT_scale=wh8_s[m][:],
+                start=True,
+                stop=False,
+                **table(0),
+            )
+        for m in range(HALVES):
+            nc.tensor.matmul_mx(
+                out=ha[m][:],
+                lhsT=wh4_w[:, 2 * m * P : 2 * (m + 1) * P].bitcast(FP4X4),
+                lhsT_scale=wh4_s[:, cols[m]],
+                start=False,
+                stop=True,
+                **table(1),
+            )
+            nc.scalar.activation(made[m][:], ha[m][:], ACT.Tanh)
+        for m in range(HALVES):
+            for a in range(PASSES):
+                nc.tensor.matmul_mx(
+                    out=ga[m][:],
+                    lhsT=wg_w[:, a, cols[m]].bitcast(FP8X4),
+                    lhsT_scale=wg_s[:, a, cols[m]],
+                    start=(a == 0),
+                    stop=(a == PASSES - 1),
+                    **table(a),
+                )
+            nc.scalar.activation(swing[m][:], ga[m][:], ACT.Tanh, bias=half_bias[:, m : m + 1], scale=0.5)
+
+        def gate(m, js):
+            nc.vector.scalar_tensor_tensor(step[m][:, js], swing[m][:, js], 1.0, diff[m][:, js], ALU.add, ALU.mult)
+
+        def finish(m, js):
+            nc.vector.scalar_tensor_tensor(result[m][:, js], step[m][:, js], 0.5, picked[m][:, js], ALU.mult, ALU.add)
+            nc.sync.dma_start(out[cols[m], js], result[m][:, js])
+
+        whole, left, right = slice(0, J), slice(0, CHUNK), slice(CHUNK, J)
+        for m in range(HALVES):
+            nc.vector.tensor_tensor(diff[m][:], made[m][:], picked[m][:], ALU.subtract)
+        gate(0, left)
+        gate(0, right)
+        finish(0, left)
+        finish(0, right)
+        gate(1, left)
+        gate(1, right)
+        finish(1, left)
+        finish(1, right)

@@ -35,23 +35,33 @@ def tile_list_hwayt_qf_tanh_kernel(
 
         held = ctx.enter_context(tc.tile_pool(name="held", bufs=1))
         offsets = held.tile([P, J // 16], U16, name="offsets")
-        tab_w0 = sb.tile([P, T], U32, name="tab_w0", align_bytes=64)
-        tab_w1 = sb.tile([P, T], U32, name="tab_w1", align_bytes=64)
+        tab_w0 = sb.tile([P, T], U32, name="tab_w0", tag="early", align_bytes=64)
+        tab_w1 = sb.tile([P, T], U32, name="tab_w1", tag="late", align_bytes=64)
         tab_w = [tab_w0, tab_w1]
-        tab_s = sb.tile([P, T], U8, name="tab_s", align_bytes=64)
+        tab_s = sb.tile([P, T], U8, name="tab_s", tag="turns", align_bytes=64)
+        wg_w = sb.tile([P, PASSES, N], U32, name="wg_w", align_bytes=64)
         wg_s = sb.tile([P, PASSES, N], U8, name="wg_s", align_bytes=64)
         wh4_w = sb.tile([P, 2 * N], U8, name="wh4_w", align_bytes=64)
         wh4_s = sb.tile([P, N], U8, name="wh4_s", align_bytes=64)
         wh8_raw = sb.tile([P, PACK, N], F32, name="wh8_raw", align_bytes=64)
         bias = sb.tile([P, HALVES], F32, name="bias")
-        half_bias = sb.tile([P, HALVES], F32, name="half_bias")
         got_s = sb.tile([P, J], U8, name="got_s", align_bytes=64)
 
-        nc.gpsimd.memset(wh4_s[:].bitcast(I32), 0)
         nc.vector.memset(wg_s[:].bitcast(I32), 0)
+        nc.vector.memset(wh4_s[:].bitcast(I32), 0)
         nc.vector.memset(tab_s[:].bitcast(I32)[32:64, :], 0)
         nc.vector.memset(tab_s[:].bitcast(I32)[64:128, :], 0)
         nc.vector.memset(got_s[:].bitcast(I32), 0)
+
+        def load_tab_scales(a):
+            first = 16 * (1 - a)
+            nc.scalar.dma_start(
+                tab_s[:].bitcast(I32)[first : first + 16, :],
+                tab_scales[a].bitcast(I32).rearrange("(q r) t -> r q t", r=4),
+            )
+
+        def load_tab_words(a):
+            nc.sync.dma_start(tab_w[a][:].bitcast(I32), tab_words[a].rearrange("p t i -> p (t i)").bitcast(I32))
 
         def load_wg_scales(engine, q):
             engine.dma_start(
@@ -59,101 +69,71 @@ def tile_list_hwayt_qf_tanh_kernel(
                 wg_scales[:, 4 * q : 4 * q + 4, :].rearrange("a r n -> r a n").bitcast(I32),
             )
 
-        def load_wh4_scales(engine, q):
-            engine.dma_start(
+        def load_wh4_scales(q):
+            nc.gpsimd.dma_start(
                 wh4_s[:].bitcast(I32)[32 * q : 32 * q + 4, :], wh4_scales[0, 4 * q : 4 * q + 4, :].bitcast(I32)
             )
 
         nc.sync.dma_start(offsets[:], offs)
-        for a, engine in enumerate((nc.sync, nc.scalar)):
-            first = 16 * (1 - a)
-            engine.dma_start(
-                tab_s[:].bitcast(I32)[first : first + 16, :],
-                tab_scales[a].bitcast(I32).rearrange("(q r) t -> r q t", r=4),
-            )
-        def load_words(a):
-            nc.sync.dma_start(tab_w[a][:].bitcast(I32), tab_words[a].rearrange("p t i -> p (t i)").bitcast(I32))
-
-        load_words(0)
+        load_tab_scales(0)
+        load_tab_words(0)
+        load_tab_scales(1)
+        with nc.allow_non_contiguous_dma(reason="one bias value for each partition and half"):
+            nc.scalar.dma_start(bias[:], bg.rearrange("(m p) -> p m", p=P))
+        nc.sync.dma_start(wg_w[:].bitcast(I32), wg_words.rearrange("a p n i -> p a (n i)").bitcast(I32))
+        load_wg_scales(nc.scalar, 0)
+        nc.sync.dma_start(wh4_w[:].bitcast(I32), wh4_words[0].bitcast(I32))
+        load_wg_scales(nc.scalar, 1)
+        load_tab_words(1)
+        load_wg_scales(nc.scalar, 2)
+        load_wg_scales(nc.gpsimd, 3)
+        for q in range(QUADS):
+            load_wh4_scales(q)
         nc.sync.dma_start(wh8_raw[:], wh8.rearrange("(p i) n -> p i n", i=PACK))
-        nc.scalar.dma_start(wh4_w[:].bitcast(I32), wh4_words[0].bitcast(I32))
-        for q, engine in enumerate((nc.scalar, nc.scalar, nc.sync, nc.gpsimd)):
-            load_wh4_scales(engine, q)
-        load_words(1)
 
         got_w = [sb.tile([P, J], U32, name=f"got_w{a}", align_bytes=64) for a in range(PASSES)]
         got_rows = sb.tile([P, J], U8, name="got_rows", align_bytes=64)
         nc.vector.tensor_copy(got_rows[:], tab_s[:].indirect(offsets[:]))
-        carry0 = sb.tile([P, T], F32, name="carry0", align_bytes=64)
-        carry1 = sb.tile([P, T], F32, name="carry1", align_bytes=64)
         for q in range(QUADS):
-            nc.sync.dma_start(
+            nc.scalar.dma_start(
                 got_s[:].bitcast(I32)[32 * q : 32 * q + 8, :], got_rows[:].bitcast(I32)[q:32:4, :]
             )
-        nc.sync.dma_start(carry0[:], rT[0:P, :])
-        nc.sync.dma_start(carry1[:], rT[P : 2 * P, :])
+        neg_bias = sb.tile([P, HALVES], F32, name="neg_bias", tag="turns", align_bytes=64)
+        nc.vector.tensor_scalar_mul(neg_bias[:], bias[:], -1.0)
         nc.vector.tensor_copy(got_w[0][:], tab_w[0][:].indirect(offsets[:]))
-        wg_w = sb.tile([P, PASSES, N], U32, name="wg_w", align_bytes=64)
-        nc.sync.dma_start(wg_w[:].bitcast(I32), wg_words.rearrange("a p n i -> p a (n i)").bitcast(I32))
-        for q in range(QUADS):
-            load_wg_scales(nc.sync, q)
-        with nc.allow_non_contiguous_dma(reason="one bias value for each partition and half"):
-            nc.sync.dma_start(bias[:], bg.rearrange("(m p) -> p m", p=P))
-        nc.scalar.mul(half_bias[:], bias[:], 0.5)
-        carry = [carry0[:], carry1[:]]
+        carry0 = sb.tile([P, T], F32, name="carry0", tag="early", align_bytes=64)
+        nc.sync.dma_start(carry0[:], rT[0:P, :])
+        nc.vector.tensor_copy(got_w[1][:], tab_w[1][:].indirect(offsets[:]))
+        carry1 = sb.tile([P, T], F32, name="carry1", tag="late", align_bytes=64)
+        nc.sync.dma_start(carry1[:], rT[P : 2 * P, :])
+        carry = [carry0, carry1]
 
-        wh8_w, wh8_s = [], []
+        cols = [slice(m * P, (m + 1) * P) for m in range(HALVES)]
+        grouped = [sb.tile([P, P, PACK], BF16, name=f"grouped{m}", align_bytes=64) for m in range(HALVES)]
+        wh8_w = [sb.tile([P, P], U32, name=f"wh8_w{m}", align_bytes=64) for m in range(HALVES)]
+        wh8_s = [sb.tile([P, P], U8, name=f"wh8_s{m}", align_bytes=64) for m in range(HALVES)]
         for m in range(HALVES):
-            grouped = sb.tile([P, P, PACK], BF16, name=f"grouped{m}", tag=f"half{m}", align_bytes=64)
-            nc.scalar.activation(
-                grouped[:].rearrange("p (c e) i -> p c i e", e=4),
-                wh8_raw[:, :, m * P : (m + 1) * P].rearrange("p i (c e) -> p c i e", e=4),
-                ACT.Copy,
+            nc.vector.tensor_copy(
+                grouped[m][:].rearrange("p (c e) i -> p c i e", e=4),
+                wh8_raw[:, :, cols[m]].rearrange("p i (c e) -> p c i e", e=4),
             )
-            words = sb.tile([P, P], U32, name=f"wh8_w{m}", align_bytes=64)
-            scales = sb.tile([P, P], U8, name=f"wh8_s{m}", align_bytes=64)
+        for m in range(HALVES):
             nc.vector.quantize_mx(
-                out=words[:].bitcast(FP8X4), scales=scales[:], in_=grouped[:].rearrange("p c i -> p (c i)")
+                out=wh8_w[m][:].bitcast(FP8X4), scales=wh8_s[m][:], in_=grouped[m][:].rearrange("p c i -> p (c i)")
             )
-            wh8_w.append(words)
-            wh8_s.append(scales)
-            if m == 0:
-                nc.vector.tensor_copy(got_w[1][:], tab_w[1][:].indirect(offsets[:]))
-
-        picked = [sb.tile([P, J], F32, name=f"picked{m}", tag=f"half{m}", align_bytes=64) for m in range(HALVES)]
-        for m in range(HALVES):
-            nc.vector.tensor_copy(picked[m][:], carry[m].indirect(offsets[:]))
 
         def table(a):
             return dict(rhs=got_w[a][:].bitcast(FP8X4), rhs_scale=got_s[TAB_ROW0[a] : P, :])
 
-        ha = [ps.tile([P, J], F32, name=f"ha{m}") for m in range(HALVES)]
         ga = [ps.tile([P, J], F32, name=f"ga{m}") for m in range(HALVES)]
-        made = [sb.tile([P, J], F32, name=f"made{m}") for m in range(HALVES)]
-        swing = [sb.tile([P, J], F32, name=f"swing{m}") for m in range(HALVES)]
-        diff = [sb.tile([P, J], F32, name=f"diff{m}") for m in range(HALVES)]
-        step = [sb.tile([P, J], F32, name=f"step{m}") for m in range(HALVES)]
+        ha = [ps.tile([P, J], F32, name=f"ha{m}") for m in range(HALVES)]
+        keep = [sb.tile([P, J], F32, name=f"keep{m}") for m in range(HALVES)]
+        made0 = sb.tile([P, J], F32, name="made0", tag="turns", align_bytes=64)
+        made1 = sb.tile([P, J], F32, name="made1", align_bytes=64)
+        made = [made0, made1]
+        kept = [sb.tile([P, J], F32, name=f"kept{m}") for m in range(HALVES)]
+        fresh = [sb.tile([P, J], F32, name=f"fresh{m}") for m in range(HALVES)]
         result = [sb.tile([P, J], F32, name=f"result{m}") for m in range(HALVES)]
-        cols = [slice(m * P, (m + 1) * P) for m in range(HALVES)]
-        for m in range(HALVES):
-            nc.tensor.matmul_mx(
-                out=ha[m][:],
-                lhsT=wh8_w[m][:].bitcast(FP8X4),
-                lhsT_scale=wh8_s[m][:],
-                start=True,
-                stop=False,
-                **table(0),
-            )
-        for m in range(HALVES):
-            nc.tensor.matmul_mx(
-                out=ha[m][:],
-                lhsT=wh4_w[:, 2 * m * P : 2 * (m + 1) * P].bitcast(FP4X4),
-                lhsT_scale=wh4_s[:, cols[m]],
-                start=False,
-                stop=True,
-                **table(1),
-            )
-            nc.scalar.activation(made[m][:], ha[m][:], ACT.Tanh)
         for m in range(HALVES):
             for a in range(PASSES):
                 nc.tensor.matmul_mx(
@@ -164,23 +144,45 @@ def tile_list_hwayt_qf_tanh_kernel(
                     stop=(a == PASSES - 1),
                     **table(a),
                 )
-            nc.scalar.activation(swing[m][:], ga[m][:], ACT.Tanh, bias=half_bias[:, m : m + 1], scale=0.5)
-
-        def gate(m, js):
-            nc.vector.scalar_tensor_tensor(step[m][:, js], swing[m][:, js], 1.0, diff[m][:, js], ALU.add, ALU.mult)
-
-        def finish(m, js):
-            nc.vector.scalar_tensor_tensor(result[m][:, js], step[m][:, js], 0.5, picked[m][:, js], ALU.mult, ALU.add)
-            nc.sync.dma_start(out[cols[m], js], result[m][:, js])
-
-        whole, left, right = slice(0, J), slice(0, CHUNK), slice(CHUNK, J)
+            nc.scalar.activation(keep[m][:], ga[m][:], ACT.Sigmoid, bias=neg_bias[:, m : m + 1], scale=-1.0)
         for m in range(HALVES):
-            nc.vector.tensor_tensor(diff[m][:], made[m][:], picked[m][:], ALU.subtract)
-        gate(0, left)
-        gate(0, right)
-        finish(0, left)
-        finish(0, right)
-        gate(1, left)
-        gate(1, right)
-        finish(1, left)
-        finish(1, right)
+            nc.tensor.matmul_mx(
+                out=ha[m][:],
+                lhsT=wh8_w[m][:].bitcast(FP8X4),
+                lhsT_scale=wh8_s[m][:],
+                start=True,
+                stop=False,
+                **table(0),
+            )
+            nc.tensor.matmul_mx(
+                out=ha[m][:],
+                lhsT=wh4_w[:, 2 * m * P : 2 * (m + 1) * P].bitcast(FP4X4),
+                lhsT_scale=wh4_s[:, cols[m]],
+                start=False,
+                stop=True,
+                **table(1),
+            )
+            nc.scalar.activation(made[m][:], ha[m][:], ACT.Tanh)
+
+        def weigh_carry(m, j0, j1):
+            window = carry[m][:].indirect(offsets[:, j0 // 16 : j1 // 16])
+            nc.vector.tensor_tensor(kept[m][:, j0:j1], window, keep[m][:, j0:j1], ALU.mult)
+
+        def weigh_made(m, j0, j1):
+            nc.vector.scalar_tensor_tensor(
+                fresh[m][:, j0:j1], keep[m][:, j0:j1], -1.0, made[m][:, j0:j1], ALU.add, ALU.mult
+            )
+
+        def finish(m, j0, j1):
+            nc.vector.tensor_tensor(result[m][:, j0:j1], kept[m][:, j0:j1], fresh[m][:, j0:j1], ALU.subtract)
+            nc.sync.dma_start(out[cols[m], j0:j1], result[m][:, j0:j1])
+
+        weigh_carry(0, 0, J)
+        weigh_carry(1, 0, CHUNK)
+        weigh_carry(1, CHUNK, J)
+        weigh_made(0, 0, J)
+        weigh_made(1, 0, CHUNK)
+        finish(0, 0, J)
+        weigh_made(1, CHUNK, J)
+        finish(1, 0, CHUNK)
+        finish(1, CHUNK, J)

@@ -35,10 +35,10 @@ def tile_list_hwayt_qf_tanh_kernel(
 
         held = ctx.enter_context(tc.tile_pool(name="held", bufs=1))
         offsets = held.tile([P, J // 16], U16, name="offsets")
-        tab_w0 = sb.tile([P, T], U32, name="tab_w0", tag="early", align_bytes=64)
-        tab_w1 = sb.tile([P, T], U32, name="tab_w1", tag="late", align_bytes=64)
+        tab_w0 = sb.tile([P, T], U32, name="tab_w0", tag="turns", align_bytes=64)
+        tab_w1 = sb.tile([P, T], U32, name="tab_w1", align_bytes=64)
         tab_w = [tab_w0, tab_w1]
-        tab_s = sb.tile([P, T], U8, name="tab_s", tag="turns", align_bytes=64)
+        tab_s = sb.tile([P, T], U8, name="tab_s", align_bytes=64)
         wg_w = sb.tile([P, PASSES, N], U32, name="wg_w", align_bytes=64)
         wg_s = sb.tile([P, PASSES, N], U8, name="wg_s", align_bytes=64)
         wh4_w = sb.tile([P, 2 * N], U8, name="wh4_w", align_bytes=64)
@@ -47,15 +47,15 @@ def tile_list_hwayt_qf_tanh_kernel(
         bias = sb.tile([P, HALVES], F32, name="bias")
         got_s = sb.tile([P, J], U8, name="got_s", align_bytes=64)
 
-        nc.vector.memset(wg_s[:].bitcast(I32), 0)
+        nc.gpsimd.memset(wg_s[:].bitcast(I32), 0)
         nc.vector.memset(wh4_s[:].bitcast(I32), 0)
         nc.vector.memset(tab_s[:].bitcast(I32)[32:64, :], 0)
         nc.vector.memset(tab_s[:].bitcast(I32)[64:128, :], 0)
         nc.vector.memset(got_s[:].bitcast(I32), 0)
 
-        def load_tab_scales(a):
+        def load_tab_scales(engine, a):
             first = 16 * (1 - a)
-            nc.scalar.dma_start(
+            engine.dma_start(
                 tab_s[:].bitcast(I32)[first : first + 16, :],
                 tab_scales[a].bitcast(I32).rearrange("(q r) t -> r q t", r=4),
             )
@@ -69,44 +69,41 @@ def tile_list_hwayt_qf_tanh_kernel(
                 wg_scales[:, 4 * q : 4 * q + 4, :].rearrange("a r n -> r a n").bitcast(I32),
             )
 
-        def load_wh4_scales(q):
-            nc.gpsimd.dma_start(
+        def load_wh4_scales(engine, q):
+            engine.dma_start(
                 wh4_s[:].bitcast(I32)[32 * q : 32 * q + 4, :], wh4_scales[0, 4 * q : 4 * q + 4, :].bitcast(I32)
             )
 
         nc.sync.dma_start(offsets[:], offs)
-        load_tab_scales(0)
-        load_tab_words(0)
-        load_tab_scales(1)
-        with nc.allow_non_contiguous_dma(reason="one bias value for each partition and half"):
-            nc.scalar.dma_start(bias[:], bg.rearrange("(m p) -> p m", p=P))
+        load_tab_scales(nc.scalar, 1)
+        load_tab_scales(nc.sync, 0)
+        for q, engine in enumerate((nc.scalar, nc.scalar, nc.gpsimd, nc.gpsimd)):
+            load_wg_scales(engine, q)
+        load_wh4_scales(nc.gpsimd, 0)
+        for a in range(PASSES):
+            load_tab_words(a)
         nc.sync.dma_start(wg_w[:].bitcast(I32), wg_words.rearrange("a p n i -> p a (n i)").bitcast(I32))
-        load_wg_scales(nc.scalar, 0)
-        nc.sync.dma_start(wh4_w[:].bitcast(I32), wh4_words[0].bitcast(I32))
-        load_wg_scales(nc.scalar, 1)
-        load_tab_words(1)
-        load_wg_scales(nc.scalar, 2)
-        load_wg_scales(nc.gpsimd, 3)
-        for q in range(QUADS):
-            load_wh4_scales(q)
         nc.sync.dma_start(wh8_raw[:], wh8.rearrange("(p i) n -> p i n", i=PACK))
+        with nc.allow_non_contiguous_dma(reason="one bias value for each partition and half"):
+            nc.sync.dma_start(bias[:], bg.rearrange("(m p) -> p m", p=P))
 
         got_w = [sb.tile([P, J], U32, name=f"got_w{a}", align_bytes=64) for a in range(PASSES)]
         got_rows = sb.tile([P, J], U8, name="got_rows", align_bytes=64)
         nc.vector.tensor_copy(got_rows[:], tab_s[:].indirect(offsets[:]))
         for q in range(QUADS):
-            nc.scalar.dma_start(
+            nc.sync.dma_start(
                 got_s[:].bitcast(I32)[32 * q : 32 * q + 8, :], got_rows[:].bitcast(I32)[q:32:4, :]
             )
+        carry = [sb.tile([P, T], F32, name=f"carry{m}", align_bytes=64) for m in range(HALVES)]
+        nc.sync.dma_start(carry[0][:], rT[0:P, :])
+        nc.sync.dma_start(carry[1][:], rT[P : 2 * P, :])
+        nc.sync.dma_start(wh4_w[:].bitcast(I32), wh4_words[0].bitcast(I32))
+        for q in range(1, QUADS):
+            load_wh4_scales(nc.sync, q)
+        nc.vector.tensor_copy(got_w[0][:], tab_w[0][:].indirect(offsets[:]))
         neg_bias = sb.tile([P, HALVES], F32, name="neg_bias", tag="turns", align_bytes=64)
         nc.vector.tensor_scalar_mul(neg_bias[:], bias[:], -1.0)
-        nc.vector.tensor_copy(got_w[0][:], tab_w[0][:].indirect(offsets[:]))
-        carry0 = sb.tile([P, T], F32, name="carry0", tag="early", align_bytes=64)
-        nc.sync.dma_start(carry0[:], rT[0:P, :])
         nc.vector.tensor_copy(got_w[1][:], tab_w[1][:].indirect(offsets[:]))
-        carry1 = sb.tile([P, T], F32, name="carry1", tag="late", align_bytes=64)
-        nc.sync.dma_start(carry1[:], rT[P : 2 * P, :])
-        carry = [carry0, carry1]
 
         cols = [slice(m * P, (m + 1) * P) for m in range(HALVES)]
         grouped = [sb.tile([P, P, PACK], BF16, name=f"grouped{m}", align_bytes=64) for m in range(HALVES)]
@@ -122,10 +119,9 @@ def tile_list_hwayt_qf_tanh_kernel(
                 out=wh8_w[m][:].bitcast(FP8X4), scales=wh8_s[m][:], in_=grouped[m][:].rearrange("p c i -> p (c i)")
             )
 
-        def table(a):
-            return dict(rhs=got_w[a][:].bitcast(FP8X4), rhs_scale=got_s[TAB_ROW0[a] : P, :])
+        def table(a, j0, j1):
+            return dict(rhs=got_w[a][:, j0:j1].bitcast(FP8X4), rhs_scale=got_s[TAB_ROW0[a] : P, j0:j1])
 
-        ga = [ps.tile([P, J], F32, name=f"ga{m}") for m in range(HALVES)]
         ha = [ps.tile([P, J], F32, name=f"ha{m}") for m in range(HALVES)]
         keep = [sb.tile([P, J], F32, name=f"keep{m}") for m in range(HALVES)]
         made0 = sb.tile([P, J], F32, name="made0", tag="turns", align_bytes=64)
@@ -134,17 +130,18 @@ def tile_list_hwayt_qf_tanh_kernel(
         kept = [sb.tile([P, J], F32, name=f"kept{m}") for m in range(HALVES)]
         fresh = [sb.tile([P, J], F32, name=f"fresh{m}") for m in range(HALVES)]
         result = [sb.tile([P, J], F32, name=f"result{m}") for m in range(HALVES)]
-        for m in range(HALVES):
+        for m, j0, j1 in ((0, 0, CHUNK), (0, CHUNK, J), (1, 0, J)):
+            ga = ps.tile([P, j1 - j0], F32, name=f"ga{m}_{j0}")
             for a in range(PASSES):
                 nc.tensor.matmul_mx(
-                    out=ga[m][:],
+                    out=ga[:],
                     lhsT=wg_w[:, a, cols[m]].bitcast(FP8X4),
                     lhsT_scale=wg_s[:, a, cols[m]],
                     start=(a == 0),
                     stop=(a == PASSES - 1),
-                    **table(a),
+                    **table(a, j0, j1),
                 )
-            nc.scalar.activation(keep[m][:], ga[m][:], ACT.Sigmoid, bias=neg_bias[:, m : m + 1], scale=-1.0)
+            nc.scalar.activation(keep[m][:, j0:j1], ga[:], ACT.Sigmoid, bias=neg_bias[:, m : m + 1], scale=-1.0)
         for m in range(HALVES):
             nc.tensor.matmul_mx(
                 out=ha[m][:],
@@ -152,7 +149,7 @@ def tile_list_hwayt_qf_tanh_kernel(
                 lhsT_scale=wh8_s[m][:],
                 start=True,
                 stop=False,
-                **table(0),
+                **table(0, 0, J),
             )
             nc.tensor.matmul_mx(
                 out=ha[m][:],
@@ -160,9 +157,10 @@ def tile_list_hwayt_qf_tanh_kernel(
                 lhsT_scale=wh4_s[:, cols[m]],
                 start=False,
                 stop=True,
-                **table(1),
+                **table(1, 0, J),
             )
-            nc.scalar.activation(made[m][:], ha[m][:], ACT.Tanh)
+        for m, j0, j1 in ((0, 0, J), (1, 0, CHUNK), (1, CHUNK, J)):
+            nc.scalar.activation(made[m][:, j0:j1], ha[m][:, j0:j1], ACT.Tanh)
 
         def weigh_carry(m, j0, j1):
             window = carry[m][:].indirect(offsets[:, j0 // 16 : j1 // 16])
@@ -177,7 +175,8 @@ def tile_list_hwayt_qf_tanh_kernel(
             nc.vector.tensor_tensor(result[m][:, j0:j1], kept[m][:, j0:j1], fresh[m][:, j0:j1], ALU.subtract)
             nc.sync.dma_start(out[cols[m], j0:j1], result[m][:, j0:j1])
 
-        weigh_carry(0, 0, J)
+        weigh_carry(0, 0, CHUNK)
+        weigh_carry(0, CHUNK, J)
         weigh_carry(1, 0, CHUNK)
         weigh_carry(1, CHUNK, J)
         weigh_made(0, 0, J)

@@ -21,8 +21,9 @@ PACK = 4
 QUADS = 4
 PASSES = 2
 HALVES = N // P
-CHUNK = 256
-TAB_ROW0 = (4, 0)
+GROUP = 16
+LEFT, RIGHT, WHOLE = slice(0, J // 2), slice(J // 2, J), slice(0, J)
+TAB_FIRST = (4, 0)
 
 
 def tile_list_hwayt_qf_tanh_kernel(
@@ -32,12 +33,10 @@ def tile_list_hwayt_qf_tanh_kernel(
     with ExitStack() as ctx:
         sb = ctx.enter_context(tc.tile_pool(name="sb", bufs=1))
         ps = ctx.enter_context(tc.psum_pool(name="ps", bufs=1))
-
         held = ctx.enter_context(tc.tile_pool(name="held", bufs=1))
-        offsets = held.tile([P, J // 16], U16, name="offsets")
-        tab_w0 = sb.tile([P, T], U32, name="tab_w0", tag="turns", align_bytes=64)
-        tab_w1 = sb.tile([P, T], U32, name="tab_w1", align_bytes=64)
-        tab_w = [tab_w0, tab_w1]
+
+        offsets = held.tile([P, J // GROUP], U16, name="offsets")
+        tab_w = [sb.tile([P, T], U32, name=f"tab_w{a}", align_bytes=64) for a in range(PASSES)]
         tab_s = sb.tile([P, T], U8, name="tab_s", align_bytes=64)
         wg_w = sb.tile([P, PASSES, N], U32, name="wg_w", align_bytes=64)
         wg_s = sb.tile([P, PASSES, N], U8, name="wg_s", align_bytes=64)
@@ -60,52 +59,48 @@ def tile_list_hwayt_qf_tanh_kernel(
                 tab_scales[a].bitcast(I32).rearrange("(q r) t -> r q t", r=4),
             )
 
-        def load_tab_words(a):
-            nc.sync.dma_start(tab_w[a][:].bitcast(I32), tab_words[a].rearrange("p t i -> p (t i)").bitcast(I32))
-
         def load_wg_scales(engine, q):
             engine.dma_start(
                 wg_s[:].bitcast(I32)[32 * q : 32 * q + 4, :, :],
                 wg_scales[:, 4 * q : 4 * q + 4, :].rearrange("a r n -> r a n").bitcast(I32),
             )
 
-        def load_wh4_scales(engine, q):
-            engine.dma_start(
-                wh4_s[:].bitcast(I32)[32 * q : 32 * q + 4, :], wh4_scales[0, 4 * q : 4 * q + 4, :].bitcast(I32)
-            )
-
         nc.sync.dma_start(offsets[:], offs)
         load_tab_scales(nc.scalar, 1)
         load_tab_scales(nc.sync, 0)
-        for q, engine in enumerate((nc.scalar, nc.scalar, nc.gpsimd, nc.gpsimd)):
-            load_wg_scales(engine, q)
-        load_wh4_scales(nc.gpsimd, 0)
+        load_wg_scales(nc.scalar, 0)
+        with nc.allow_non_contiguous_dma(reason="one bias value for each partition and half"):
+            nc.scalar.dma_start(bias[:], bg.rearrange("(m p) -> p m", p=P))
+        load_wg_scales(nc.scalar, 1)
+        for q in range(2, QUADS):
+            load_wg_scales(nc.gpsimd, q)
         for a in range(PASSES):
-            load_tab_words(a)
+            nc.sync.dma_start(tab_w[a][:].bitcast(I32), tab_words[a].rearrange("p t i -> p (t i)").bitcast(I32))
         nc.sync.dma_start(wg_w[:].bitcast(I32), wg_words.rearrange("a p n i -> p a (n i)").bitcast(I32))
         nc.sync.dma_start(wh8_raw[:], wh8.rearrange("(p i) n -> p i n", i=PACK))
-        with nc.allow_non_contiguous_dma(reason="one bias value for each partition and half"):
-            nc.sync.dma_start(bias[:], bg.rearrange("(m p) -> p m", p=P))
 
-        got_w = [sb.tile([P, J], U32, name=f"got_w{a}", align_bytes=64) for a in range(PASSES)]
         got_rows = sb.tile([P, J], U8, name="got_rows", align_bytes=64)
         nc.vector.tensor_copy(got_rows[:], tab_s[:].indirect(offsets[:]))
         for q in range(QUADS):
-            nc.sync.dma_start(
-                got_s[:].bitcast(I32)[32 * q : 32 * q + 8, :], got_rows[:].bitcast(I32)[q:32:4, :]
-            )
-        carry = [sb.tile([P, T], F32, name=f"carry{m}", align_bytes=64) for m in range(HALVES)]
-        nc.sync.dma_start(carry[0][:], rT[0:P, :])
-        nc.sync.dma_start(carry[1][:], rT[P : 2 * P, :])
-        nc.sync.dma_start(wh4_w[:].bitcast(I32), wh4_words[0].bitcast(I32))
-        for q in range(1, QUADS):
-            load_wh4_scales(nc.sync, q)
-        nc.vector.tensor_copy(got_w[0][:], tab_w[0][:].indirect(offsets[:]))
-        neg_bias = sb.tile([P, HALVES], F32, name="neg_bias", tag="turns", align_bytes=64)
-        nc.vector.tensor_scalar_mul(neg_bias[:], bias[:], -1.0)
-        nc.vector.tensor_copy(got_w[1][:], tab_w[1][:].indirect(offsets[:]))
+            nc.sync.dma_start(got_s[:].bitcast(I32)[32 * q : 32 * q + 8, :], got_rows[:].bitcast(I32)[q:32:4, :])
 
         cols = [slice(m * P, (m + 1) * P) for m in range(HALVES)]
+        carry = [sb.tile([P, T], F32, name=f"carry{m}", align_bytes=64) for m in range(HALVES)]
+        for m in range(HALVES):
+            nc.sync.dma_start(carry[m][:], rT[cols[m], :])
+        nc.sync.dma_start(wh4_w[:].bitcast(I32), wh4_words[0].bitcast(I32))
+        for q in range(QUADS):
+            nc.sync.dma_start(
+                wh4_s[:].bitcast(I32)[32 * q : 32 * q + 4, :], wh4_scales[0, 4 * q : 4 * q + 4, :].bitcast(I32)
+            )
+
+        neg_bias = sb.tile([P, HALVES], F32, name="neg_bias", tag="bias_then_made", align_bytes=64)
+        nc.vector.tensor_scalar_mul(neg_bias[:], bias[:], -1.0)
+
+        got_w = [sb.tile([P, J], U32, name=f"got_w{a}", align_bytes=64) for a in range(PASSES)]
+        for a in range(PASSES):
+            nc.vector.tensor_copy(got_w[a][:], tab_w[a][:].indirect(offsets[:]))
+
         grouped = [sb.tile([P, P, PACK], BF16, name=f"grouped{m}", align_bytes=64) for m in range(HALVES)]
         wh8_w = [sb.tile([P, P], U32, name=f"wh8_w{m}", align_bytes=64) for m in range(HALVES)]
         wh8_s = [sb.tile([P, P], U8, name=f"wh8_s{m}", align_bytes=64) for m in range(HALVES)]
@@ -119,29 +114,34 @@ def tile_list_hwayt_qf_tanh_kernel(
                 out=wh8_w[m][:].bitcast(FP8X4), scales=wh8_s[m][:], in_=grouped[m][:].rearrange("p c i -> p (c i)")
             )
 
-        def table(a, j0, j1):
-            return dict(rhs=got_w[a][:, j0:j1].bitcast(FP8X4), rhs_scale=got_s[TAB_ROW0[a] : P, j0:j1])
+        def table(a, js):
+            return dict(rhs=got_w[a][:, js].bitcast(FP8X4), rhs_scale=got_s[TAB_FIRST[a] : P, js])
 
-        ha = [ps.tile([P, J], F32, name=f"ha{m}") for m in range(HALVES)]
-        keep = [sb.tile([P, J], F32, name=f"keep{m}") for m in range(HALVES)]
-        made0 = sb.tile([P, J], F32, name="made0", tag="turns", align_bytes=64)
-        made1 = sb.tile([P, J], F32, name="made1", align_bytes=64)
-        made = [made0, made1]
-        kept = [sb.tile([P, J], F32, name=f"kept{m}") for m in range(HALVES)]
-        fresh = [sb.tile([P, J], F32, name=f"fresh{m}") for m in range(HALVES)]
-        result = [sb.tile([P, J], F32, name=f"result{m}") for m in range(HALVES)]
-        for m, j0, j1 in ((0, 0, CHUNK), (0, CHUNK, J), (1, 0, J)):
-            ga = ps.tile([P, j1 - j0], F32, name=f"ga{m}_{j0}")
+        def gate_sum(m, js, name):
+            acc = ps.tile([P, js.stop - js.start], F32, name=name)
             for a in range(PASSES):
                 nc.tensor.matmul_mx(
-                    out=ga[:],
+                    out=acc[:],
                     lhsT=wg_w[:, a, cols[m]].bitcast(FP8X4),
                     lhsT_scale=wg_s[:, a, cols[m]],
                     start=(a == 0),
                     stop=(a == PASSES - 1),
-                    **table(a, j0, j1),
+                    **table(a, js),
                 )
-            nc.scalar.activation(keep[m][:, j0:j1], ga[:], ACT.Sigmoid, bias=neg_bias[:, m : m + 1], scale=-1.0)
+            return acc
+
+        keep = [sb.tile([P, J], F32, name=f"keep{m}") for m in range(HALVES)]
+
+        def make_keep(m, js, ga):
+            nc.scalar.activation(keep[m][:, js], ga, ACT.Sigmoid, bias=neg_bias[:, m : m + 1], scale=-1.0)
+
+        make_keep(0, LEFT, gate_sum(0, LEFT, "ga0_left")[:])
+        make_keep(0, RIGHT, gate_sum(0, RIGHT, "ga0_right")[:])
+        ga1 = gate_sum(1, WHOLE, "ga1")
+        for js in (LEFT, RIGHT):
+            make_keep(1, js, ga1[:, js])
+
+        ha = [ps.tile([P, J], F32, name=f"ha{m}") for m in range(HALVES)]
         for m in range(HALVES):
             nc.tensor.matmul_mx(
                 out=ha[m][:],
@@ -149,7 +149,7 @@ def tile_list_hwayt_qf_tanh_kernel(
                 lhsT_scale=wh8_s[m][:],
                 start=True,
                 stop=False,
-                **table(0, 0, J),
+                **table(0, WHOLE),
             )
             nc.tensor.matmul_mx(
                 out=ha[m][:],
@@ -157,31 +157,35 @@ def tile_list_hwayt_qf_tanh_kernel(
                 lhsT_scale=wh4_s[:, cols[m]],
                 start=False,
                 stop=True,
-                **table(1, 0, J),
+                **table(1, WHOLE),
             )
-        for m, j0, j1 in ((0, 0, J), (1, 0, CHUNK), (1, CHUNK, J)):
-            nc.scalar.activation(made[m][:, j0:j1], ha[m][:, j0:j1], ACT.Tanh)
+        made0 = sb.tile([P, J], F32, name="made0", tag="bias_then_made", align_bytes=64)
+        made1 = sb.tile([P, J], F32, name="made1", align_bytes=64)
+        made = [made0, made1]
+        for m, js in ((0, WHOLE), (1, LEFT), (1, RIGHT)):
+            nc.scalar.activation(made[m][:, js], ha[m][:, js], ACT.Tanh)
 
-        def weigh_carry(m, j0, j1):
-            window = carry[m][:].indirect(offsets[:, j0 // 16 : j1 // 16])
-            nc.vector.tensor_tensor(kept[m][:, j0:j1], window, keep[m][:, j0:j1], ALU.mult)
+        kept = [sb.tile([P, J], F32, name=f"kept{m}") for m in range(HALVES)]
+        minus_new = [sb.tile([P, J], F32, name=f"minus_new{m}") for m in range(HALVES)]
+        result = [sb.tile([P, J], F32, name=f"result{m}") for m in range(HALVES)]
 
-        def weigh_made(m, j0, j1):
-            nc.vector.scalar_tensor_tensor(
-                fresh[m][:, j0:j1], keep[m][:, j0:j1], -1.0, made[m][:, j0:j1], ALU.add, ALU.mult
-            )
+        def weigh_carry(m, js):
+            picked = carry[m][:].indirect(offsets[:, js.start // GROUP : js.stop // GROUP])
+            nc.vector.tensor_tensor(kept[m][:, js], picked, keep[m][:, js], ALU.mult)
 
-        def finish(m, j0, j1):
-            nc.vector.tensor_tensor(result[m][:, j0:j1], kept[m][:, j0:j1], fresh[m][:, j0:j1], ALU.subtract)
-            nc.sync.dma_start(out[cols[m], j0:j1], result[m][:, j0:j1])
+        def weigh_made(m, js):
+            nc.vector.scalar_tensor_tensor(minus_new[m][:, js], keep[m][:, js], -1.0, made[m][:, js], ALU.add, ALU.mult)
 
-        weigh_carry(0, 0, CHUNK)
-        weigh_carry(0, CHUNK, J)
-        weigh_carry(1, 0, CHUNK)
-        weigh_carry(1, CHUNK, J)
-        weigh_made(0, 0, J)
-        weigh_made(1, 0, CHUNK)
-        finish(0, 0, J)
-        weigh_made(1, CHUNK, J)
-        finish(1, 0, CHUNK)
-        finish(1, CHUNK, J)
+        def finish(m, js):
+            nc.vector.tensor_tensor(result[m][:, js], kept[m][:, js], minus_new[m][:, js], ALU.subtract)
+            nc.sync.dma_start(out[cols[m], js], result[m][:, js])
+
+        for m in range(HALVES):
+            for js in (LEFT, RIGHT):
+                weigh_carry(m, js)
+        weigh_made(0, WHOLE)
+        weigh_made(1, LEFT)
+        finish(0, WHOLE)
+        weigh_made(1, RIGHT)
+        finish(1, LEFT)
+        finish(1, RIGHT)

@@ -23,7 +23,8 @@ PASSES = 2
 HALVES = N // P
 GROUP = 16
 LEFT, RIGHT, WHOLE = slice(0, J // 2), slice(J // 2, J), slice(0, J)
-TAB_FIRST = (4, 0)
+FIRST = (4, 0)
+TAB_AT, WG_AT, WH4_AT, SCALE_COLS = 0, J, J + N, J + 2 * N
 
 
 def tile_list_hwayt_qf_tanh_kernel(
@@ -35,157 +36,156 @@ def tile_list_hwayt_qf_tanh_kernel(
         ps = ctx.enter_context(tc.psum_pool(name="ps", bufs=1))
         held = ctx.enter_context(tc.tile_pool(name="held", bufs=1))
 
+        cols = [slice(m * P, (m + 1) * P) for m in range(HALVES)]
         offsets = held.tile([P, J // GROUP], U16, name="offsets")
         tab_w = [sb.tile([P, T], U32, name=f"tab_w{a}", align_bytes=64) for a in range(PASSES)]
         tab_s = sb.tile([P, T], U8, name="tab_s", align_bytes=64)
-        wg_w = sb.tile([P, PASSES, N], U32, name="wg_w", align_bytes=64)
-        wg_s = sb.tile([P, PASSES, N], U8, name="wg_s", align_bytes=64)
+        wg_w = [sb.tile([P, PASSES, P], U32, name=f"wg_w{m}", align_bytes=64) for m in range(HALVES)]
         wh4_w = sb.tile([P, 2 * N], U8, name="wh4_w", align_bytes=64)
-        wh4_s = sb.tile([P, N], U8, name="wh4_s", align_bytes=64)
         wh8_raw = sb.tile([P, PACK, N], F32, name="wh8_raw", align_bytes=64)
+        carry = [sb.tile([P, T], F32, name=f"carry{m}", align_bytes=64) for m in range(HALVES)]
         bias = sb.tile([P, HALVES], F32, name="bias")
-        got_s = sb.tile([P, J], U8, name="got_s", align_bytes=64)
+        neg_bias = sb.tile([P, HALVES], F32, name="neg_bias")
+        rows = sb.tile([32, SCALE_COLS // 4], I32, name="rows", align_bytes=64)
+        scales = sb.tile([P, SCALE_COLS], U8, name="scales", align_bytes=64)
+        warm = sb.tile([P, 8], F32, name="warm")
 
-        nc.gpsimd.memset(wg_s[:].bitcast(I32), 0)
-        nc.vector.memset(wh4_s[:].bitcast(I32), 0)
+        nc.vector.memset(rows[:, WH4_AT // 4 :], 0)
+        nc.vector.memset(warm[:], 0.0)
         nc.vector.memset(tab_s[:].bitcast(I32)[32:64, :], 0)
         nc.vector.memset(tab_s[:].bitcast(I32)[64:128, :], 0)
-        nc.vector.memset(got_s[:].bitcast(I32), 0)
+        nc.vector.memset(scales[:].bitcast(I32), 0)
 
-        def load_tab_scales(engine, a):
+        def load_rows(engine, tile, source, a):
             first = 16 * (1 - a)
-            engine.dma_start(
-                tab_s[:].bitcast(I32)[first : first + 16, :],
-                tab_scales[a].bitcast(I32).rearrange("(q r) t -> r q t", r=4),
-            )
+            engine.dma_start(tile[first : first + 16, :], source.bitcast(I32).rearrange("(q r) t -> r q t", r=4))
 
-        def load_wg_scales(engine, q):
-            engine.dma_start(
-                wg_s[:].bitcast(I32)[32 * q : 32 * q + 4, :, :],
-                wg_scales[:, 4 * q : 4 * q + 4, :].rearrange("a r n -> r a n").bitcast(I32),
-            )
+        with nc.allow_non_contiguous_dma(reason="one bias value for each partition and half"):
+            nc.gpsimd.dma_start(bias[:], bg.rearrange("(m p) -> p m", p=P))
+        nc.gpsimd.tensor_scalar(neg_bias[:], bias[:], -1.0, 0.0, ALU.mult, ALU.add)
 
         nc.sync.dma_start(offsets[:], offs)
-        load_tab_scales(nc.scalar, 1)
-        load_tab_scales(nc.sync, 0)
-        load_wg_scales(nc.scalar, 0)
-        with nc.allow_non_contiguous_dma(reason="one bias value for each partition and half"):
-            nc.scalar.dma_start(bias[:], bg.rearrange("(m p) -> p m", p=P))
-        load_wg_scales(nc.scalar, 1)
-        for q in range(2, QUADS):
-            load_wg_scales(nc.gpsimd, q)
+        load_rows(nc.scalar, tab_s[:].bitcast(I32), tab_scales[1], 1)
+        load_rows(nc.sync, tab_s[:].bitcast(I32), tab_scales[0], 0)
         for a in range(PASSES):
+            load_rows(nc.scalar, rows[:, WG_AT // 4 : WH4_AT // 4], wg_scales[a], a)
+
+        def load_words(a):
             nc.sync.dma_start(tab_w[a][:].bitcast(I32), tab_words[a].rearrange("p t i -> p (t i)").bitcast(I32))
-        nc.sync.dma_start(wg_w[:].bitcast(I32), wg_words.rearrange("a p n i -> p a (n i)").bitcast(I32))
+
+        load_words(0)
+        load_rows(nc.sync, rows[:, WH4_AT // 4 :], wh4_scales[0], 1)
+        load_words(1)
+
+        def load_wg(m):
+            words = wg_words.rearrange("a p n i -> p a (n i)").bitcast(I32)
+            nc.sync.dma_start(wg_w[m][:].bitcast(I32), words[:, :, cols[m]])
+
         nc.sync.dma_start(wh8_raw[:], wh8.rearrange("(p i) n -> p i n", i=PACK))
-
-        got_rows = sb.tile([P, J], U8, name="got_rows", align_bytes=64)
-        nc.vector.tensor_copy(got_rows[:], tab_s[:].indirect(offsets[:]))
-        for q in range(QUADS):
-            nc.sync.dma_start(got_s[:].bitcast(I32)[32 * q : 32 * q + 8, :], got_rows[:].bitcast(I32)[q:32:4, :])
-
-        cols = [slice(m * P, (m + 1) * P) for m in range(HALVES)]
-        carry = [sb.tile([P, T], F32, name=f"carry{m}", align_bytes=64) for m in range(HALVES)]
-        for m in range(HALVES):
-            nc.sync.dma_start(carry[m][:], rT[cols[m], :])
+        load_wg(0)
         nc.sync.dma_start(wh4_w[:].bitcast(I32), wh4_words[0].bitcast(I32))
-        for q in range(QUADS):
-            nc.sync.dma_start(
-                wh4_s[:].bitcast(I32)[32 * q : 32 * q + 4, :], wh4_scales[0, 4 * q : 4 * q + 4, :].bitcast(I32)
-            )
 
-        neg_bias = sb.tile([P, HALVES], F32, name="neg_bias", tag="bias_then_made", align_bytes=64)
-        nc.vector.tensor_scalar_mul(neg_bias[:], bias[:], -1.0)
+        nc.scalar.activation(warm[:, 4:8], warm[:, 0:4], ACT.Sigmoid)
+
+        got_s = sb.tile([P, J], U8, name="got_s", align_bytes=64)
+        nc.vector.tensor_copy(got_s[:], tab_s[:].indirect(offsets[:]))
+        nc.vector.tensor_copy(rows[:, : J // 4], got_s[:].bitcast(I32)[0:32, :])
+        for q in range(QUADS):
+            engine = nc.sync if q % 2 else nc.scalar
+            engine.dma_start(scales[:].bitcast(I32)[32 * q : 32 * q + 8, :], rows[q:32:4, :])
+
+        nc.sync.dma_start(carry[0][:], rT[cols[0], :])
+        load_wg(1)
+        nc.sync.dma_start(carry[1][:], rT[cols[1], :])
+
+        def picks(js):
+            return offsets[:, js.start // GROUP : js.stop // GROUP]
 
         got_w = [sb.tile([P, J], U32, name=f"got_w{a}", align_bytes=64) for a in range(PASSES)]
-        for a in range(PASSES):
-            nc.vector.tensor_copy(got_w[a][:], tab_w[a][:].indirect(offsets[:]))
+        for js in (slice(0, P), slice(P, J)):
+            nc.vector.tensor_copy(got_w[0][:, js], tab_w[0][:].indirect(picks(js)))
+        for js in (LEFT, RIGHT):
+            nc.vector.tensor_copy(got_w[1][:, js], tab_w[1][:].indirect(picks(js)))
 
         grouped = [sb.tile([P, P, PACK], BF16, name=f"grouped{m}", align_bytes=64) for m in range(HALVES)]
         wh8_w = [sb.tile([P, P], U32, name=f"wh8_w{m}", align_bytes=64) for m in range(HALVES)]
         wh8_s = [sb.tile([P, P], U8, name=f"wh8_s{m}", align_bytes=64) for m in range(HALVES)]
-        for m in range(HALVES):
-            nc.vector.tensor_copy(
+        keep = [sb.tile([P, J], F32, name=f"keep{m}") for m in range(HALVES)]
+        made = [sb.tile([P, J], F32, name=f"made{m}") for m in range(HALVES)]
+        kept = [sb.tile([P, J], F32, name=f"kept{m}") for m in range(HALVES)]
+        result = [sb.tile([P, J], F32, name=f"result{m}") for m in range(HALVES)]
+
+        def round_wh8(m):
+            nc.scalar.copy(
                 grouped[m][:].rearrange("p (c e) i -> p c i e", e=4),
                 wh8_raw[:, :, cols[m]].rearrange("p i (c e) -> p c i e", e=4),
             )
-        for m in range(HALVES):
+
+        def quantise_wh8(m):
             nc.vector.quantize_mx(
                 out=wh8_w[m][:].bitcast(FP8X4), scales=wh8_s[m][:], in_=grouped[m][:].rearrange("p c i -> p (c i)")
             )
 
         def table(a, js):
-            return dict(rhs=got_w[a][:, js].bitcast(FP8X4), rhs_scale=got_s[TAB_FIRST[a] : P, js])
+            return dict(rhs=got_w[a][:, js].bitcast(FP8X4), rhs_scale=scales[FIRST[a] : P, js])
 
-        def gate_sum(m, js, name):
-            acc = ps.tile([P, js.stop - js.start], F32, name=name)
+        def make_keep(m, js):
+            acc = ps.tile([P, js.stop - js.start], F32, name=f"ga{m}_{js.start}", tag=f"bank_g{m}_{js.start}")
             for a in range(PASSES):
                 nc.tensor.matmul_mx(
                     out=acc[:],
-                    lhsT=wg_w[:, a, cols[m]].bitcast(FP8X4),
-                    lhsT_scale=wg_s[:, a, cols[m]],
+                    lhsT=wg_w[m][:, a, :].bitcast(FP8X4),
+                    lhsT_scale=scales[FIRST[a] : P, WG_AT + m * P : WG_AT + (m + 1) * P],
                     start=(a == 0),
                     stop=(a == PASSES - 1),
                     **table(a, js),
                 )
-            return acc
+            nc.scalar.activation(keep[m][:, js], acc[:], ACT.Sigmoid, bias=neg_bias[:, m : m + 1], scale=-1.0)
 
-        keep = [sb.tile([P, J], F32, name=f"keep{m}") for m in range(HALVES)]
-
-        def make_keep(m, js, ga):
-            nc.scalar.activation(keep[m][:, js], ga, ACT.Sigmoid, bias=neg_bias[:, m : m + 1], scale=-1.0)
-
-        make_keep(0, LEFT, gate_sum(0, LEFT, "ga0_left")[:])
-        make_keep(0, RIGHT, gate_sum(0, RIGHT, "ga0_right")[:])
-        ga1 = gate_sum(1, WHOLE, "ga1")
-        for js in (LEFT, RIGHT):
-            make_keep(1, js, ga1[:, js])
-
-        ha = [ps.tile([P, J], F32, name=f"ha{m}") for m in range(HALVES)]
-        for m in range(HALVES):
+        def make_new(m, js):
+            acc = ps.tile([P, js.stop - js.start], F32, name=f"ha{m}_{js.start}", tag=f"bank_{'hg'[m]}{m}_{js.start}")
             nc.tensor.matmul_mx(
-                out=ha[m][:],
+                out=acc[:],
                 lhsT=wh8_w[m][:].bitcast(FP8X4),
                 lhsT_scale=wh8_s[m][:],
                 start=True,
                 stop=False,
-                **table(0, WHOLE),
+                **table(0, js),
             )
-            nc.tensor.matmul_mx(
-                out=ha[m][:],
-                lhsT=wh4_w[:, 2 * m * P : 2 * (m + 1) * P].bitcast(FP4X4),
-                lhsT_scale=wh4_s[:, cols[m]],
-                start=False,
-                stop=True,
-                **table(1, WHOLE),
-            )
-        made0 = sb.tile([P, J], F32, name="made0", tag="bias_then_made", align_bytes=64)
-        made1 = sb.tile([P, J], F32, name="made1", align_bytes=64)
-        made = [made0, made1]
-        for m, js in ((0, WHOLE), (1, LEFT), (1, RIGHT)):
-            nc.scalar.activation(made[m][:, js], ha[m][:, js], ACT.Tanh)
-
-        kept = [sb.tile([P, J], F32, name=f"kept{m}") for m in range(HALVES)]
-        minus_new = [sb.tile([P, J], F32, name=f"minus_new{m}") for m in range(HALVES)]
-        result = [sb.tile([P, J], F32, name=f"result{m}") for m in range(HALVES)]
+            for j0 in range(js.start, js.stop, P):
+                nc.tensor.matmul_mx(
+                    out=acc[:, j0 - js.start : j0 - js.start + P],
+                    lhsT=wh4_w[:, 2 * m * P : 2 * (m + 1) * P].bitcast(FP4X4),
+                    lhsT_scale=scales[:, WH4_AT + m * P : WH4_AT + (m + 1) * P],
+                    start=False,
+                    stop=(j0 + P == js.stop),
+                    **table(1, slice(j0, j0 + P)),
+                )
+            nc.scalar.activation(made[m][:, js], acc[:], ACT.Tanh)
 
         def weigh_carry(m, js):
-            picked = carry[m][:].indirect(offsets[:, js.start // GROUP : js.stop // GROUP])
-            nc.vector.tensor_tensor(kept[m][:, js], picked, keep[m][:, js], ALU.mult)
+            nc.vector.tensor_tensor(kept[m][:, js], carry[m][:].indirect(picks(js)), keep[m][:, js], ALU.mult)
 
         def weigh_made(m, js):
-            nc.vector.scalar_tensor_tensor(minus_new[m][:, js], keep[m][:, js], -1.0, made[m][:, js], ALU.add, ALU.mult)
+            nc.vector.scalar_tensor_tensor(keep[m][:, js], keep[m][:, js], -1.0, made[m][:, js], ALU.add, ALU.mult)
 
         def finish(m, js):
-            nc.vector.tensor_tensor(result[m][:, js], kept[m][:, js], minus_new[m][:, js], ALU.subtract)
+            nc.vector.tensor_tensor(result[m][:, js], kept[m][:, js], keep[m][:, js], ALU.subtract)
             nc.sync.dma_start(out[cols[m], js], result[m][:, js])
 
         for m in range(HALVES):
+            round_wh8(m)
+        for m in range(HALVES):
+            quantise_wh8(m)
+        for m in range(HALVES):
+            for js in (LEFT, RIGHT):
+                make_keep(m, js)
+            for js in (LEFT, RIGHT):
+                make_new(m, js)
+        for m in range(HALVES):
             for js in (LEFT, RIGHT):
                 weigh_carry(m, js)
-        weigh_made(0, WHOLE)
-        weigh_made(1, LEFT)
-        finish(0, WHOLE)
-        weigh_made(1, RIGHT)
-        finish(1, LEFT)
-        finish(1, RIGHT)
+            for js in (LEFT, RIGHT):
+                weigh_made(m, js)
+            for js in (LEFT, RIGHT):
+                finish(m, js)

@@ -40,18 +40,16 @@ def tile_list_hwayt_qf_tanh_kernel(
         offsets = held.tile([P, J // GROUP], U16, name="offsets")
         tab_w = [sb.tile([P, T], U32, name=f"tab_w{a}", align_bytes=64) for a in range(PASSES)]
         tab_s = sb.tile([P, T], U8, name="tab_s", align_bytes=64)
-        wg_w = [sb.tile([P, PASSES, P], U32, name=f"wg_w{m}", align_bytes=64) for m in range(HALVES)]
+        wg_w = sb.tile([P, PASSES, N], U32, name="wg_w", align_bytes=64)
         wh4_w = sb.tile([P, 2 * N], U8, name="wh4_w", align_bytes=64)
         wh8_raw = sb.tile([P, PACK, N], F32, name="wh8_raw", align_bytes=64)
         carry = [sb.tile([P, T], F32, name=f"carry{m}", align_bytes=64) for m in range(HALVES)]
         bias = sb.tile([P, HALVES], F32, name="bias")
-        neg_bias = sb.tile([P, HALVES], F32, name="neg_bias")
+        half_bias = sb.tile([P, HALVES], F32, name="half_bias")
         rows = sb.tile([32, SCALE_COLS // 4], I32, name="rows", align_bytes=64)
         scales = sb.tile([P, SCALE_COLS], U8, name="scales", align_bytes=64)
-        warm = sb.tile([P, 8], F32, name="warm")
 
         nc.vector.memset(rows[:, WH4_AT // 4 :], 0)
-        nc.vector.memset(warm[:], 0.0)
         nc.vector.memset(tab_s[:].bitcast(I32)[32:64, :], 0)
         nc.vector.memset(tab_s[:].bitcast(I32)[64:128, :], 0)
         nc.vector.memset(scales[:].bitcast(I32), 0)
@@ -59,10 +57,6 @@ def tile_list_hwayt_qf_tanh_kernel(
         def load_rows(engine, tile, source, a):
             first = 16 * (1 - a)
             engine.dma_start(tile[first : first + 16, :], source.bitcast(I32).rearrange("(q r) t -> r q t", r=4))
-
-        with nc.allow_non_contiguous_dma(reason="one bias value for each partition and half"):
-            nc.gpsimd.dma_start(bias[:], bg.rearrange("(m p) -> p m", p=P))
-        nc.gpsimd.tensor_scalar(neg_bias[:], bias[:], -1.0, 0.0, ALU.mult, ALU.add)
 
         nc.sync.dma_start(offsets[:], offs)
         load_rows(nc.scalar, tab_s[:].bitcast(I32), tab_scales[1], 1)
@@ -76,16 +70,8 @@ def tile_list_hwayt_qf_tanh_kernel(
         load_words(0)
         load_rows(nc.sync, rows[:, WH4_AT // 4 :], wh4_scales[0], 1)
         load_words(1)
-
-        def load_wg(m):
-            words = wg_words.rearrange("a p n i -> p a (n i)").bitcast(I32)
-            nc.sync.dma_start(wg_w[m][:].bitcast(I32), words[:, :, cols[m]])
-
         nc.sync.dma_start(wh8_raw[:], wh8.rearrange("(p i) n -> p i n", i=PACK))
-        load_wg(0)
         nc.sync.dma_start(wh4_w[:].bitcast(I32), wh4_words[0].bitcast(I32))
-
-        nc.scalar.activation(warm[:, 4:8], warm[:, 0:4], ACT.Sigmoid)
 
         got_s = sb.tile([P, J], U8, name="got_s", align_bytes=64)
         nc.vector.tensor_copy(got_s[:], tab_s[:].indirect(offsets[:]))
@@ -94,9 +80,11 @@ def tile_list_hwayt_qf_tanh_kernel(
             engine = nc.sync if q % 2 else nc.scalar
             engine.dma_start(scales[:].bitcast(I32)[32 * q : 32 * q + 8, :], rows[q:32:4, :])
 
-        nc.sync.dma_start(carry[0][:], rT[cols[0], :])
-        load_wg(1)
-        nc.sync.dma_start(carry[1][:], rT[cols[1], :])
+        for m in range(HALVES):
+            nc.sync.dma_start(carry[m][:], rT[cols[m], :])
+        nc.sync.dma_start(wg_w[:].bitcast(I32), wg_words.rearrange("a p n i -> p a (n i)").bitcast(I32))
+        with nc.allow_non_contiguous_dma(reason="one bias value for each partition and half"):
+            nc.sync.dma_start(bias[:], bg.rearrange("(m p) -> p m", p=P))
 
         def picks(js):
             return offsets[:, js.start // GROUP : js.stop // GROUP]
@@ -116,7 +104,8 @@ def tile_list_hwayt_qf_tanh_kernel(
         result = [sb.tile([P, J], F32, name=f"result{m}") for m in range(HALVES)]
 
         def round_wh8(m):
-            nc.scalar.copy(
+            copy = nc.scalar.copy if m else nc.vector.tensor_copy
+            copy(
                 grouped[m][:].rearrange("p (c e) i -> p c i e", e=4),
                 wh8_raw[:, :, cols[m]].rearrange("p i (c e) -> p c i e", e=4),
             )
@@ -130,62 +119,65 @@ def tile_list_hwayt_qf_tanh_kernel(
             return dict(rhs=got_w[a][:, js].bitcast(FP8X4), rhs_scale=scales[FIRST[a] : P, js])
 
         def make_keep(m, js):
-            acc = ps.tile([P, js.stop - js.start], F32, name=f"ga{m}_{js.start}", tag=f"bank_g{m}_{js.start}")
+            acc = ps.tile([P, js.stop - js.start], F32, name=f"ga{m}_{js.start}")
             for a in range(PASSES):
                 nc.tensor.matmul_mx(
                     out=acc[:],
-                    lhsT=wg_w[m][:, a, :].bitcast(FP8X4),
+                    lhsT=wg_w[:, a, cols[m]].bitcast(FP8X4),
                     lhsT_scale=scales[FIRST[a] : P, WG_AT + m * P : WG_AT + (m + 1) * P],
                     start=(a == 0),
                     stop=(a == PASSES - 1),
                     **table(a, js),
                 )
-            nc.scalar.activation(keep[m][:, js], acc[:], ACT.Sigmoid, bias=neg_bias[:, m : m + 1], scale=-1.0)
+            nc.scalar.activation(keep[m][:, js], acc[:], ACT.Tanh, bias=half_bias[:, m : m + 1], scale=0.5)
 
         def make_new(m, js):
-            acc = ps.tile([P, js.stop - js.start], F32, name=f"ha{m}_{js.start}", tag=f"bank_{'hg'[m]}{m}_{js.start}")
-            nc.tensor.matmul_mx(
-                out=acc[:],
-                lhsT=wh8_w[m][:].bitcast(FP8X4),
-                lhsT_scale=wh8_s[m][:],
-                start=True,
-                stop=False,
-                **table(0, js),
-            )
+            acc = ps.tile([P, js.stop - js.start], F32, name=f"ha{m}_{js.start}")
             for j0 in range(js.start, js.stop, P):
                 nc.tensor.matmul_mx(
                     out=acc[:, j0 - js.start : j0 - js.start + P],
                     lhsT=wh4_w[:, 2 * m * P : 2 * (m + 1) * P].bitcast(FP4X4),
                     lhsT_scale=scales[:, WH4_AT + m * P : WH4_AT + (m + 1) * P],
-                    start=False,
-                    stop=(j0 + P == js.stop),
+                    start=(j0 == js.start),
+                    stop=False,
                     **table(1, slice(j0, j0 + P)),
                 )
+            nc.tensor.matmul_mx(
+                out=acc[:],
+                lhsT=wh8_w[m][:].bitcast(FP8X4),
+                lhsT_scale=wh8_s[m][:],
+                start=False,
+                stop=True,
+                **table(0, js),
+            )
             nc.scalar.activation(made[m][:, js], acc[:], ACT.Tanh)
 
         def weigh_carry(m, js):
-            nc.vector.tensor_tensor(kept[m][:, js], carry[m][:].indirect(picks(js)), keep[m][:, js], ALU.mult)
+            nc.vector.tensor_tensor(kept[m][:, js], carry[m][:].indirect(picks(js)), made[m][:, js], ALU.subtract)
 
         def weigh_made(m, js):
-            nc.vector.scalar_tensor_tensor(keep[m][:, js], keep[m][:, js], -1.0, made[m][:, js], ALU.add, ALU.mult)
+            nc.vector.scalar_tensor_tensor(keep[m][:, js], keep[m][:, js], -1.0, kept[m][:, js], ALU.add, ALU.mult)
 
         def finish(m, js):
-            nc.vector.tensor_tensor(result[m][:, js], kept[m][:, js], keep[m][:, js], ALU.subtract)
+            nc.vector.scalar_tensor_tensor(result[m][:, js], keep[m][:, js], -0.5, made[m][:, js], ALU.mult, ALU.add)
             nc.sync.dma_start(out[cols[m], js], result[m][:, js])
 
         for m in range(HALVES):
             round_wh8(m)
         for m in range(HALVES):
             quantise_wh8(m)
-        for m in range(HALVES):
-            for js in (LEFT, RIGHT):
-                make_keep(m, js)
-            for js in (LEFT, RIGHT):
-                make_new(m, js)
-        for m in range(HALVES):
-            for js in (LEFT, RIGHT):
-                weigh_carry(m, js)
-            for js in (LEFT, RIGHT):
-                weigh_made(m, js)
-            for js in (LEFT, RIGHT):
-                finish(m, js)
+        quarters = [(m, js) for m in range(HALVES) for js in (LEFT, RIGHT)]
+        for m, js in quarters:
+            make_new(m, js)
+        nc.scalar.mul(half_bias[:], bias[:], 0.5)
+        for m, js in quarters:
+            make_keep(m, js)
+        for m, js in quarters:
+            weigh_carry(m, js)
+        weigh_made(0, LEFT)
+        weigh_made(0, RIGHT)
+        weigh_made(1, LEFT)
+        finish(0, WHOLE)
+        weigh_made(1, RIGHT)
+        finish(1, LEFT)
+        finish(1, RIGHT)

@@ -24,7 +24,6 @@ HALVES = N // P
 GROUP = 16
 LEFT, RIGHT, WHOLE = slice(0, J // 2), slice(J // 2, J), slice(0, J)
 FIRST = (4, 0)
-TAB_AT, WG_AT, WH4_AT, SCALE_COLS = 0, J, J + N, J + 2 * N
 
 
 def tile_list_hwayt_qf_tanh_kernel(
@@ -38,73 +37,105 @@ def tile_list_hwayt_qf_tanh_kernel(
 
         cols = [slice(m * P, (m + 1) * P) for m in range(HALVES)]
         offsets = held.tile([P, J // GROUP], U16, name="offsets")
-        tab_w = [sb.tile([P, T], U32, name=f"tab_w{a}", align_bytes=64) for a in range(PASSES)]
+        tab_w = [sb.tile([P, T], U32, name=f"tab_w{a}", tag=f"window{a}", align_bytes=64) for a in range(PASSES)]
         tab_s = sb.tile([P, T], U8, name="tab_s", align_bytes=64)
         wg_w = sb.tile([P, PASSES, N], U32, name="wg_w", align_bytes=64)
         wh4_w = sb.tile([P, 2 * N], U8, name="wh4_w", align_bytes=64)
         wh8_raw = sb.tile([P, PACK, N], F32, name="wh8_raw", align_bytes=64)
         carry = [sb.tile([P, T], F32, name=f"carry{m}", align_bytes=64) for m in range(HALVES)]
         bias = sb.tile([P, HALVES], F32, name="bias")
-        half_bias = sb.tile([P, HALVES], F32, name="half_bias")
-        rows = sb.tile([32, SCALE_COLS // 4], I32, name="rows", align_bytes=64)
-        scales = sb.tile([P, SCALE_COLS], U8, name="scales", align_bytes=64)
+        scales = sb.tile([P, J], U8, name="scales", align_bytes=64)
+        wg_s = sb.tile([P, N], U8, name="wg_s", align_bytes=64)
+        wh4_s = sb.tile([P, N], U8, name="wh4_s", align_bytes=64)
 
-        nc.vector.memset(rows[:, WH4_AT // 4 :], 0)
+        nc.gpsimd.memset(wh4_s[:].bitcast(I32), 0)
         nc.vector.memset(tab_s[:].bitcast(I32)[32:64, :], 0)
         nc.vector.memset(tab_s[:].bitcast(I32)[64:128, :], 0)
         nc.vector.memset(scales[:].bitcast(I32), 0)
+        nc.vector.memset(wg_s[:].bitcast(I32), 0)
+
+        def load_wh4_scales(engine, q):
+            engine.dma_start(
+                wh4_s[:].bitcast(I32)[32 * q : 32 * q + 4, :], wh4_scales[0, 4 * q : 4 * q + 4, :].bitcast(I32)
+            )
+
+        def load_wg_scales(engine, q):
+            engine.dma_start(
+                wg_s[:].bitcast(I32)[32 * q : 32 * q + 8, :], wg_scales[:, 4 * q : 4 * q + 4, :].bitcast(I32)
+            )
 
         def load_rows(engine, tile, source, a):
             first = 16 * (1 - a)
             engine.dma_start(tile[first : first + 16, :], source.bitcast(I32).rearrange("(q r) t -> r q t", r=4))
 
-        nc.sync.dma_start(offsets[:], offs)
-        load_rows(nc.scalar, tab_s[:].bitcast(I32), tab_scales[1], 1)
-        load_rows(nc.sync, tab_s[:].bitcast(I32), tab_scales[0], 0)
-        for a in range(PASSES):
-            load_rows(nc.scalar, rows[:, WG_AT // 4 : WH4_AT // 4], wg_scales[a], a)
-
         def load_words(a):
             nc.sync.dma_start(tab_w[a][:].bitcast(I32), tab_words[a].rearrange("p t i -> p (t i)").bitcast(I32))
 
+        def load_wg():
+            nc.sync.dma_start(wg_w[:].bitcast(I32), wg_words.rearrange("a p n i -> p a (n i)").bitcast(I32))
+
+        def load_carry(m):
+            nc.sync.dma_start(carry[m][:], rT[cols[m], :])
+
+        def load_wh8():
+            nc.sync.dma_start(wh8_raw[:], wh8.rearrange("(p i) n -> p i n", i=PACK))
+
+        def load_bias(engine):
+            with nc.allow_non_contiguous_dma(reason="one bias value for each partition and half"):
+                engine.dma_start(bias[:], bg.rearrange("(m p) -> p m", p=P))
+
+        def load_wh4():
+            nc.sync.dma_start(wh4_w[:].bitcast(I32), wh4_words[0].bitcast(I32))
+
+        nc.sync.dma_start(offsets[:], offs)
+        load_rows(nc.scalar, tab_s[:].bitcast(I32), tab_scales[1], 1)
+        load_rows(nc.sync, tab_s[:].bitcast(I32), tab_scales[0], 0)
+        for q in range(QUADS):
+            load_wh4_scales(nc.scalar if q < 2 else nc.gpsimd, q)
+        warm = sb.tile([P, 2], F32, name="warm")
+        nc.gpsimd.memset(warm[:, 0:1], 0.0)
+        nc.scalar.activation(warm[:, 1:2], warm[:, 0:1], ACT.Sigmoid)
         load_words(0)
-        load_rows(nc.sync, rows[:, WH4_AT // 4 :], wh4_scales[0], 1)
         load_words(1)
-        nc.sync.dma_start(wh8_raw[:], wh8.rearrange("(p i) n -> p i n", i=PACK))
-        nc.sync.dma_start(wh4_w[:].bitcast(I32), wh4_words[0].bitcast(I32))
+        load_wh8()
+        load_wh4()
 
         got_s = sb.tile([P, J], U8, name="got_s", align_bytes=64)
         nc.vector.tensor_copy(got_s[:], tab_s[:].indirect(offsets[:]))
-        nc.vector.tensor_copy(rows[:, : J // 4], got_s[:].bitcast(I32)[0:32, :])
         for q in range(QUADS):
             engine = nc.sync if q % 2 else nc.scalar
-            engine.dma_start(scales[:].bitcast(I32)[32 * q : 32 * q + 8, :], rows[q:32:4, :])
-
-        for m in range(HALVES):
-            nc.sync.dma_start(carry[m][:], rT[cols[m], :])
-        nc.sync.dma_start(wg_w[:].bitcast(I32), wg_words.rearrange("a p n i -> p a (n i)").bitcast(I32))
-        with nc.allow_non_contiguous_dma(reason="one bias value for each partition and half"):
-            nc.sync.dma_start(bias[:], bg.rearrange("(m p) -> p m", p=P))
+            engine.dma_start(scales[:].bitcast(I32)[32 * q : 32 * q + 8, :], got_s[:].bitcast(I32)[q:32:4, :])
+        load_carry(0)
+        load_carry(1)
+        load_wg()
+        for q in range(QUADS):
+            load_wg_scales(nc.sync, q)
+        load_bias(nc.sync)
 
         def picks(js):
             return offsets[:, js.start // GROUP : js.stop // GROUP]
 
-        got_w = [sb.tile([P, J], U32, name=f"got_w{a}", align_bytes=64) for a in range(PASSES)]
-        for js in (slice(0, P), slice(P, J)):
-            nc.vector.tensor_copy(got_w[0][:, js], tab_w[0][:].indirect(picks(js)))
-        for js in (LEFT, RIGHT):
-            nc.vector.tensor_copy(got_w[1][:, js], tab_w[1][:].indirect(picks(js)))
-
-        grouped = [sb.tile([P, P, PACK], BF16, name=f"grouped{m}", align_bytes=64) for m in range(HALVES)]
-        wh8_w = [sb.tile([P, P], U32, name=f"wh8_w{m}", align_bytes=64) for m in range(HALVES)]
+        grouped = [
+            sb.tile([P, P, PACK], BF16, name=f"grouped{m}", tag=f"grouped{m}", align_bytes=64) for m in range(HALVES)
+        ]
+        got_w = [
+            sb.tile([P, J], U32, name="got_w0", align_bytes=64),
+            sb.tile([P, J], U32, name="got_w1", align_bytes=64),
+        ]
+        wh8_w = [
+            sb.tile([P, P], U32, name="wh8_w0", align_bytes=64),
+            sb.tile([P, P], U32, name="wh8_w1", align_bytes=64),
+        ]
         wh8_s = [sb.tile([P, P], U8, name=f"wh8_s{m}", align_bytes=64) for m in range(HALVES)]
-        keep = [sb.tile([P, J], F32, name=f"keep{m}") for m in range(HALVES)]
+        gate = [sb.tile([P, J], F32, name=f"gate{m}") for m in range(HALVES)]
         made = [sb.tile([P, J], F32, name=f"made{m}") for m in range(HALVES)]
-        kept = [sb.tile([P, J], F32, name=f"kept{m}") for m in range(HALVES)]
+        diff = [sb.tile([P, J], F32, name=f"diff{m}") for m in range(HALVES)]
         result = [sb.tile([P, J], F32, name=f"result{m}") for m in range(HALVES)]
 
-        def round_wh8(m):
-            copy = nc.scalar.copy if m else nc.vector.tensor_copy
+        def gather_words(a, js):
+            nc.vector.tensor_copy(got_w[a][:, js], tab_w[a][:].indirect(picks(js)))
+
+        def round_wh8(m, copy):
             copy(
                 grouped[m][:].rearrange("p (c e) i -> p c i e", e=4),
                 wh8_raw[:, :, cols[m]].rearrange("p i (c e) -> p c i e", e=4),
@@ -118,30 +149,40 @@ def tile_list_hwayt_qf_tanh_kernel(
         def table(a, js):
             return dict(rhs=got_w[a][:, js].bitcast(FP8X4), rhs_scale=scales[FIRST[a] : P, js])
 
-        def make_keep(m, js):
+        def within(js, part):
+            return slice(part.start - js.start, part.stop - js.start)
+
+        def make_gate(m, js, parts):
             acc = ps.tile([P, js.stop - js.start], F32, name=f"ga{m}_{js.start}")
             for a in range(PASSES):
                 nc.tensor.matmul_mx(
                     out=acc[:],
                     lhsT=wg_w[:, a, cols[m]].bitcast(FP8X4),
-                    lhsT_scale=scales[FIRST[a] : P, WG_AT + m * P : WG_AT + (m + 1) * P],
+                    lhsT_scale=wg_s[4 * a : P, cols[m]],
                     start=(a == 0),
                     stop=(a == PASSES - 1),
                     **table(a, js),
                 )
-            nc.scalar.activation(keep[m][:, js], acc[:], ACT.Tanh, bias=half_bias[:, m : m + 1], scale=0.5)
+            for part in parts:
+                nc.scalar.activation(gate[m][:, part], acc[:, within(js, part)], ACT.Sigmoid, bias=bias[:, m : m + 1])
 
-        def make_new(m, js):
+        ha = {}
+
+        def open_new(m, js):
             acc = ps.tile([P, js.stop - js.start], F32, name=f"ha{m}_{js.start}")
+            ha[m, js.start] = acc
             for j0 in range(js.start, js.stop, P):
                 nc.tensor.matmul_mx(
                     out=acc[:, j0 - js.start : j0 - js.start + P],
                     lhsT=wh4_w[:, 2 * m * P : 2 * (m + 1) * P].bitcast(FP4X4),
-                    lhsT_scale=scales[:, WH4_AT + m * P : WH4_AT + (m + 1) * P],
+                    lhsT_scale=wh4_s[:, cols[m]],
                     start=(j0 == js.start),
                     stop=False,
                     **table(1, slice(j0, j0 + P)),
                 )
+
+        def close_new(m, js):
+            acc = ha[m, js.start]
             nc.tensor.matmul_mx(
                 out=acc[:],
                 lhsT=wh8_w[m][:].bitcast(FP8X4),
@@ -152,32 +193,51 @@ def tile_list_hwayt_qf_tanh_kernel(
             )
             nc.scalar.activation(made[m][:, js], acc[:], ACT.Tanh)
 
-        def weigh_carry(m, js):
-            nc.vector.tensor_tensor(kept[m][:, js], carry[m][:].indirect(picks(js)), made[m][:, js], ALU.subtract)
+        def differ(m, js):
+            nc.vector.tensor_tensor(diff[m][:, js], carry[m][:].indirect(picks(js)), made[m][:, js], ALU.subtract)
 
-        def weigh_made(m, js):
-            nc.vector.scalar_tensor_tensor(keep[m][:, js], keep[m][:, js], -1.0, kept[m][:, js], ALU.add, ALU.mult)
+        picked = sb.tile([P, J // 2], F32, name="picked")
+
+        def pick_right():
+            nc.vector.tensor_copy(picked[:], carry[0][:].indirect(picks(RIGHT)))
+
+        def differ_right():
+            nc.vector.tensor_tensor(diff[0][:, RIGHT], picked[:], made[0][:, RIGHT], ALU.subtract)
+
+        def weigh(m, js):
+            nc.vector.scalar_tensor_tensor(gate[m][:, js], gate[m][:, js], -1.0, diff[m][:, js], ALU.add, ALU.mult)
 
         def finish(m, js):
-            nc.vector.scalar_tensor_tensor(result[m][:, js], keep[m][:, js], -0.5, made[m][:, js], ALU.mult, ALU.add)
-            nc.sync.dma_start(out[cols[m], js], result[m][:, js])
+            nc.vector.tensor_tensor(result[m][:, js], made[m][:, js], gate[m][:, js], ALU.subtract)
 
-        for m in range(HALVES):
-            round_wh8(m)
-        for m in range(HALVES):
-            quantise_wh8(m)
-        quarters = [(m, js) for m in range(HALVES) for js in (LEFT, RIGHT)]
-        for m, js in quarters:
-            make_new(m, js)
-        nc.scalar.mul(half_bias[:], bias[:], 0.5)
-        for m, js in quarters:
-            make_keep(m, js)
-        for m, js in quarters:
-            weigh_carry(m, js)
-        weigh_made(0, LEFT)
-        weigh_made(0, RIGHT)
-        weigh_made(1, LEFT)
+        def store(m, js, engine):
+            engine.dma_start(out[cols[m], js], result[m][:, js])
+
+        gather_words(0, WHOLE)
+        gather_words(1, LEFT)
+        gather_words(1, RIGHT)
+        round_wh8(0, nc.scalar.copy)
+        round_wh8(1, nc.vector.tensor_copy)
+        quantise_wh8(0)
+        quantise_wh8(1)
+        for m, js in ((0, LEFT), (0, RIGHT), (1, LEFT), (1, RIGHT)):
+            open_new(m, js)
+            close_new(m, js)
+        make_gate(0, LEFT, [LEFT])
+        make_gate(0, RIGHT, [RIGHT])
+        make_gate(1, WHOLE, [LEFT, RIGHT])
+        pick_right()
+        differ(0, LEFT)
+        differ_right()
+        differ(1, LEFT)
+        differ(1, RIGHT)
+        weigh(0, LEFT)
+        weigh(0, RIGHT)
+        weigh(1, LEFT)
         finish(0, WHOLE)
-        weigh_made(1, RIGHT)
+        store(0, WHOLE, nc.sync)
+        weigh(1, RIGHT)
         finish(1, LEFT)
+        store(1, LEFT, nc.sync)
         finish(1, RIGHT)
+        store(1, RIGHT, nc.scalar)

@@ -23,7 +23,9 @@ PASSES = 2
 HALVES = N // P
 GROUP = 16
 LEFT, RIGHT, WHOLE = slice(0, J // 2), slice(J // 2, J), slice(0, J)
+EARLY, NEXT = slice(0, P), slice(P, 2 * P)
 FIRST = (4, 0)
+WG_AT, WH4_AT, SCALE_COLS = J, J + N, J + 2 * N
 
 
 def tile_list_hwayt_qf_tanh_kernel(
@@ -39,30 +41,19 @@ def tile_list_hwayt_qf_tanh_kernel(
         offsets = held.tile([P, J // GROUP], U16, name="offsets")
         tab_w = [sb.tile([P, T], U32, name=f"tab_w{a}", tag=f"window{a}", align_bytes=64) for a in range(PASSES)]
         tab_s = sb.tile([P, T], U8, name="tab_s", align_bytes=64)
-        wg_w = sb.tile([P, PASSES, N], U32, name="wg_w", align_bytes=64)
+        wg_w = [sb.tile([P, PASSES, P], U32, name=f"wg_w{m}", align_bytes=64) for m in range(HALVES)]
         wh4_w = sb.tile([P, 2 * N], U8, name="wh4_w", align_bytes=64)
         wh8_raw = sb.tile([P, PACK, N], F32, name="wh8_raw", align_bytes=64)
         carry = [sb.tile([P, T], F32, name=f"carry{m}", align_bytes=64) for m in range(HALVES)]
         bias = sb.tile([P, HALVES], F32, name="bias")
-        scales = sb.tile([P, J], U8, name="scales", align_bytes=64)
-        wg_s = sb.tile([P, N], U8, name="wg_s", align_bytes=64)
-        wh4_s = sb.tile([P, N], U8, name="wh4_s", align_bytes=64)
+        half_bias = sb.tile([P, HALVES], F32, name="half_bias")
+        rows = sb.tile([32, SCALE_COLS // 4], I32, name="rows", align_bytes=64)
+        scales = sb.tile([P, SCALE_COLS], U8, name="scales", align_bytes=64)
 
-        nc.gpsimd.memset(wh4_s[:].bitcast(I32), 0)
+        nc.vector.memset(rows[:, WH4_AT // 4 :], 0)
         nc.vector.memset(tab_s[:].bitcast(I32)[32:64, :], 0)
         nc.vector.memset(tab_s[:].bitcast(I32)[64:128, :], 0)
         nc.vector.memset(scales[:].bitcast(I32), 0)
-        nc.vector.memset(wg_s[:].bitcast(I32), 0)
-
-        def load_wh4_scales(engine, q):
-            engine.dma_start(
-                wh4_s[:].bitcast(I32)[32 * q : 32 * q + 4, :], wh4_scales[0, 4 * q : 4 * q + 4, :].bitcast(I32)
-            )
-
-        def load_wg_scales(engine, q):
-            engine.dma_start(
-                wg_s[:].bitcast(I32)[32 * q : 32 * q + 8, :], wg_scales[:, 4 * q : 4 * q + 4, :].bitcast(I32)
-            )
 
         def load_rows(engine, tile, source, a):
             first = 16 * (1 - a)
@@ -71,8 +62,10 @@ def tile_list_hwayt_qf_tanh_kernel(
         def load_words(a):
             nc.sync.dma_start(tab_w[a][:].bitcast(I32), tab_words[a].rearrange("p t i -> p (t i)").bitcast(I32))
 
-        def load_wg():
-            nc.sync.dma_start(wg_w[:].bitcast(I32), wg_words.rearrange("a p n i -> p a (n i)").bitcast(I32))
+        def load_wg(m):
+            nc.sync.dma_start(
+                wg_w[m][:].bitcast(I32), wg_words[:, :, cols[m], :].rearrange("a p n i -> p a (n i)").bitcast(I32)
+            )
 
         def load_carry(m):
             nc.sync.dma_start(carry[m][:], rT[cols[m], :])
@@ -90,27 +83,24 @@ def tile_list_hwayt_qf_tanh_kernel(
         nc.sync.dma_start(offsets[:], offs)
         load_rows(nc.scalar, tab_s[:].bitcast(I32), tab_scales[1], 1)
         load_rows(nc.sync, tab_s[:].bitcast(I32), tab_scales[0], 0)
-        for q in range(QUADS):
-            load_wh4_scales(nc.scalar if q < 2 else nc.gpsimd, q)
-        warm = sb.tile([P, 2], F32, name="warm")
-        nc.gpsimd.memset(warm[:, 0:1], 0.0)
-        nc.scalar.activation(warm[:, 1:2], warm[:, 0:1], ACT.Sigmoid)
+        for a in range(PASSES):
+            load_rows(nc.scalar, rows[:, WG_AT // 4 : WH4_AT // 4], wg_scales[a], a)
         load_words(0)
-        load_words(1)
+        load_rows(nc.sync, rows[:, WH4_AT // 4 :], wh4_scales[0], 1)
         load_wh8()
+        load_words(1)
         load_wh4()
 
         got_s = sb.tile([P, J], U8, name="got_s", align_bytes=64)
         nc.vector.tensor_copy(got_s[:], tab_s[:].indirect(offsets[:]))
+        nc.vector.tensor_copy(rows[:, : J // 4], got_s[:].bitcast(I32)[0:32, :])
         for q in range(QUADS):
-            engine = nc.sync if q % 2 else nc.scalar
-            engine.dma_start(scales[:].bitcast(I32)[32 * q : 32 * q + 8, :], got_s[:].bitcast(I32)[q:32:4, :])
+            nc.sync.dma_start(scales[:].bitcast(I32)[32 * q : 32 * q + 8, :], rows[q:32:4, :])
         load_carry(0)
+        load_wg(0)
         load_carry(1)
-        load_wg()
-        for q in range(QUADS):
-            load_wg_scales(nc.sync, q)
         load_bias(nc.sync)
+        load_wg(1)
 
         def picks(js):
             return offsets[:, js.start // GROUP : js.stop // GROUP]
@@ -120,7 +110,6 @@ def tile_list_hwayt_qf_tanh_kernel(
         ]
         got_w = [
             sb.tile([P, J], U32, name="got_w0", align_bytes=64),
-            sb.tile([P, J], U32, name="got_w1", align_bytes=64),
         ]
         wh8_w = [
             sb.tile([P, P], U32, name="wh8_w0", align_bytes=64),
@@ -153,86 +142,71 @@ def tile_list_hwayt_qf_tanh_kernel(
             return slice(part.start - js.start, part.stop - js.start)
 
         def make_gate(m, js, parts):
-            acc = ps.tile([P, js.stop - js.start], F32, name=f"ga{m}_{js.start}")
+            tag = "ha0_0" if (m, js) == (1, RIGHT) else f"ga{m}_{js.start}"
+            acc = ps.tile([P, js.stop - js.start], F32, name=f"ga{m}_{js.start}", tag=tag)
             for a in range(PASSES):
                 nc.tensor.matmul_mx(
                     out=acc[:],
-                    lhsT=wg_w[:, a, cols[m]].bitcast(FP8X4),
-                    lhsT_scale=wg_s[4 * a : P, cols[m]],
+                    lhsT=wg_w[m][:, a, :].bitcast(FP8X4),
+                    lhsT_scale=scales[FIRST[a] : P, WG_AT + m * P : WG_AT + (m + 1) * P],
                     start=(a == 0),
                     stop=(a == PASSES - 1),
                     **table(a, js),
                 )
             for part in parts:
-                nc.scalar.activation(gate[m][:, part], acc[:, within(js, part)], ACT.Sigmoid, bias=bias[:, m : m + 1])
+                nc.scalar.activation(gate[m][:, part], acc[:, within(js, part)], ACT.Tanh, bias=half_bias[:, m : m + 1], scale=0.5)
 
-        ha = {}
-
-        def open_new(m, js):
-            acc = ps.tile([P, js.stop - js.start], F32, name=f"ha{m}_{js.start}")
-            ha[m, js.start] = acc
-            for j0 in range(js.start, js.stop, P):
-                nc.tensor.matmul_mx(
-                    out=acc[:, j0 - js.start : j0 - js.start + P],
-                    lhsT=wh4_w[:, 2 * m * P : 2 * (m + 1) * P].bitcast(FP4X4),
-                    lhsT_scale=wh4_s[:, cols[m]],
-                    start=(j0 == js.start),
-                    stop=False,
-                    **table(1, slice(j0, j0 + P)),
-                )
-
-        def close_new(m, js):
-            acc = ha[m, js.start]
+        def make_new(m, js):
+            acc = ps.tile([P, js.stop - js.start], F32, name=f"ha{m}_{js.start}", tag=f"ha{m}_{js.start}")
             nc.tensor.matmul_mx(
                 out=acc[:],
                 lhsT=wh8_w[m][:].bitcast(FP8X4),
                 lhsT_scale=wh8_s[m][:],
-                start=False,
-                stop=True,
+                start=True,
+                stop=False,
                 **table(0, js),
             )
+            for j0 in range(js.start, js.stop, P):
+                nc.tensor.matmul_mx(
+                    out=acc[:, j0 - js.start : j0 - js.start + P],
+                    lhsT=wh4_w[:, 2 * m * P : 2 * (m + 1) * P].bitcast(FP4X4),
+                    lhsT_scale=scales[:, WH4_AT + m * P : WH4_AT + (m + 1) * P],
+                    start=False,
+                    stop=(j0 + P == js.stop),
+                    **table(1, slice(j0, j0 + P)),
+                )
             nc.scalar.activation(made[m][:, js], acc[:], ACT.Tanh)
 
         def differ(m, js):
             nc.vector.tensor_tensor(diff[m][:, js], carry[m][:].indirect(picks(js)), made[m][:, js], ALU.subtract)
 
-        picked = sb.tile([P, J // 2], F32, name="picked")
-
-        def pick_right():
-            nc.vector.tensor_copy(picked[:], carry[0][:].indirect(picks(RIGHT)))
-
-        def differ_right():
-            nc.vector.tensor_tensor(diff[0][:, RIGHT], picked[:], made[0][:, RIGHT], ALU.subtract)
-
         def weigh(m, js):
             nc.vector.scalar_tensor_tensor(gate[m][:, js], gate[m][:, js], -1.0, diff[m][:, js], ALU.add, ALU.mult)
 
         def finish(m, js):
-            nc.vector.tensor_tensor(result[m][:, js], made[m][:, js], gate[m][:, js], ALU.subtract)
+            nc.vector.scalar_tensor_tensor(result[m][:, js], gate[m][:, js], -0.5, made[m][:, js], ALU.mult, ALU.add)
 
         def store(m, js, engine):
             engine.dma_start(out[cols[m], js], result[m][:, js])
 
         gather_words(0, WHOLE)
-        gather_words(1, LEFT)
-        gather_words(1, RIGHT)
         round_wh8(0, nc.scalar.copy)
-        round_wh8(1, nc.vector.tensor_copy)
+        round_wh8(1, nc.scalar.copy)
         quantise_wh8(0)
+        got_w.append(sb.tile([P, J], U32, name="got_w1", tag="grouped0", align_bytes=64))
+        for js in (EARLY, NEXT, RIGHT):
+            gather_words(1, js)
         quantise_wh8(1)
-        for m, js in ((0, LEFT), (0, RIGHT), (1, LEFT), (1, RIGHT)):
-            open_new(m, js)
-            close_new(m, js)
-        make_gate(0, LEFT, [LEFT])
-        make_gate(0, RIGHT, [RIGHT])
-        make_gate(1, WHOLE, [LEFT, RIGHT])
-        pick_right()
-        differ(0, LEFT)
-        differ_right()
-        differ(1, LEFT)
-        differ(1, RIGHT)
-        weigh(0, LEFT)
-        weigh(0, RIGHT)
+        quarters = [(m, js) for m in range(HALVES) for js in (LEFT, RIGHT)]
+        pieces = [(0, EARLY), (0, NEXT)] + quarters[1:]
+        for m, js in pieces:
+            make_new(m, js)
+        nc.scalar.mul(half_bias[:], bias[:], 0.5)
+        for m, js in quarters:
+            make_gate(m, js, [js])
+        for m, js in pieces:
+            differ(m, js)
+        weigh(0, WHOLE)
         weigh(1, LEFT)
         finish(0, WHOLE)
         store(0, WHOLE, nc.sync)
@@ -240,4 +214,4 @@ def tile_list_hwayt_qf_tanh_kernel(
         finish(1, LEFT)
         store(1, LEFT, nc.sync)
         finish(1, RIGHT)
-        store(1, RIGHT, nc.scalar)
+        store(1, RIGHT, nc.sync)

@@ -19,7 +19,9 @@ ALU = mybir.AluOpType
 P = 128
 PACK = 4
 QUADS = 4
+QUAD = P // QUADS
 PASSES = 2
+BLOCKS = 16
 HALVES = N // P
 GROUP = 16
 LEFT, RIGHT, WHOLE = slice(0, J // 2), slice(J // 2, J), slice(0, J)
@@ -39,7 +41,7 @@ def tile_list_hwayt_qf_tanh_kernel(
 
         cols = [slice(m * P, (m + 1) * P) for m in range(HALVES)]
         offsets = held.tile([P, J // GROUP], U16, name="offsets")
-        tab_w = [sb.tile([P, T], U32, name=f"tab_w{a}", tag=f"window{a}", align_bytes=64) for a in range(PASSES)]
+        tab_w = [sb.tile([P, T], U32, name=f"tab_w{a}", align_bytes=64) for a in range(PASSES)]
         tab_s = sb.tile([P, T], U8, name="tab_s", align_bytes=64)
         wg_w = [sb.tile([P, PASSES, P], U32, name=f"wg_w{m}", align_bytes=64) for m in range(HALVES)]
         wh4_w = sb.tile([P, 2 * N], U8, name="wh4_w", align_bytes=64)
@@ -47,17 +49,19 @@ def tile_list_hwayt_qf_tanh_kernel(
         carry = [sb.tile([P, T], F32, name=f"carry{m}", align_bytes=64) for m in range(HALVES)]
         bias = sb.tile([P, HALVES], F32, name="bias")
         half_bias = sb.tile([P, HALVES], F32, name="half_bias")
-        rows = sb.tile([32, SCALE_COLS // 4], I32, name="rows", align_bytes=64)
+        rows = sb.tile([PASSES * BLOCKS, SCALE_COLS // PACK], I32, name="rows", align_bytes=64)
         scales = sb.tile([P, SCALE_COLS], U8, name="scales", align_bytes=64)
 
-        nc.vector.memset(rows[:, WH4_AT // 4 :], 0)
-        nc.vector.memset(tab_s[:].bitcast(I32)[32:64, :], 0)
-        nc.vector.memset(tab_s[:].bitcast(I32)[64:128, :], 0)
+        nc.vector.memset(rows[:, WH4_AT // PACK :], 0)
+        nc.vector.memset(tab_s[:].bitcast(I32)[QUAD : 2 * QUAD, :], 0)
+        nc.vector.memset(tab_s[:].bitcast(I32)[2 * QUAD : P, :], 0)
         nc.vector.memset(scales[:].bitcast(I32), 0)
 
         def load_rows(engine, tile, source, a):
-            first = 16 * (1 - a)
-            engine.dma_start(tile[first : first + 16, :], source.bitcast(I32).rearrange("(q r) t -> r q t", r=4))
+            first = BLOCKS * (1 - a)
+            engine.dma_start(
+                tile[first : first + BLOCKS, :], source.bitcast(I32).rearrange("(q r) t -> r q t", q=QUADS)
+            )
 
         def load_words(a):
             nc.sync.dma_start(tab_w[a][:].bitcast(I32), tab_words[a].rearrange("p t i -> p (t i)").bitcast(I32))
@@ -67,39 +71,30 @@ def tile_list_hwayt_qf_tanh_kernel(
                 wg_w[m][:].bitcast(I32), wg_words[:, :, cols[m], :].rearrange("a p n i -> p a (n i)").bitcast(I32)
             )
 
-        def load_carry(m):
-            nc.sync.dma_start(carry[m][:], rT[cols[m], :])
-
-        def load_wh8():
-            nc.sync.dma_start(wh8_raw[:], wh8.rearrange("(p i) n -> p i n", i=PACK))
-
-        def load_bias(engine):
-            with nc.allow_non_contiguous_dma(reason="one bias value for each partition and half"):
-                engine.dma_start(bias[:], bg.rearrange("(m p) -> p m", p=P))
-
-        def load_wh4():
-            nc.sync.dma_start(wh4_w[:].bitcast(I32), wh4_words[0].bitcast(I32))
-
         nc.sync.dma_start(offsets[:], offs)
         load_rows(nc.scalar, tab_s[:].bitcast(I32), tab_scales[1], 1)
         load_rows(nc.sync, tab_s[:].bitcast(I32), tab_scales[0], 0)
         for a in range(PASSES):
-            load_rows(nc.scalar, rows[:, WG_AT // 4 : WH4_AT // 4], wg_scales[a], a)
+            load_rows(nc.scalar, rows[:, WG_AT // PACK : WH4_AT // PACK], wg_scales[a], a)
         load_words(0)
-        load_rows(nc.sync, rows[:, WH4_AT // 4 :], wh4_scales[0], 1)
-        load_wh8()
+        load_rows(nc.sync, rows[:, WH4_AT // PACK :], wh4_scales[0], 1)
+        nc.sync.dma_start(wh8_raw[:], wh8.rearrange("(p i) n -> p i n", i=PACK))
         load_words(1)
-        load_wh4()
+        nc.sync.dma_start(wh4_w[:].bitcast(I32), wh4_words[0].bitcast(I32))
 
         got_s = sb.tile([P, J], U8, name="got_s", align_bytes=64)
         nc.vector.tensor_copy(got_s[:], tab_s[:].indirect(offsets[:]))
-        nc.vector.tensor_copy(rows[:, : J // 4], got_s[:].bitcast(I32)[0:32, :])
+        nc.vector.tensor_copy(rows[:, : J // PACK], got_s[:].bitcast(I32)[0 : PASSES * BLOCKS, :])
         for q in range(QUADS):
-            nc.sync.dma_start(scales[:].bitcast(I32)[32 * q : 32 * q + 8, :], rows[q:32:4, :])
-        load_carry(0)
+            nc.sync.dma_start(
+                scales[:].bitcast(I32)[QUAD * q : QUAD * q + PASSES * BLOCKS // QUADS, :],
+                rows[q : PASSES * BLOCKS : QUADS, :],
+            )
+        nc.sync.dma_start(carry[0][:], rT[cols[0], :])
         load_wg(0)
-        load_carry(1)
-        load_bias(nc.sync)
+        nc.sync.dma_start(carry[1][:], rT[cols[1], :])
+        with nc.allow_non_contiguous_dma(reason="one bias value for each partition and half"):
+            nc.sync.dma_start(bias[:], bg.rearrange("(m p) -> p m", p=P))
         load_wg(1)
 
         def picks(js):
@@ -108,13 +103,8 @@ def tile_list_hwayt_qf_tanh_kernel(
         grouped = [
             sb.tile([P, P, PACK], BF16, name=f"grouped{m}", tag=f"grouped{m}", align_bytes=64) for m in range(HALVES)
         ]
-        got_w = [
-            sb.tile([P, J], U32, name="got_w0", align_bytes=64),
-        ]
-        wh8_w = [
-            sb.tile([P, P], U32, name="wh8_w0", align_bytes=64),
-            sb.tile([P, P], U32, name="wh8_w1", align_bytes=64),
-        ]
+        got_w = [sb.tile([P, J], U32, name="got_w0", align_bytes=64)]
+        wh8_w = [sb.tile([P, P], U32, name=f"wh8_w{m}", align_bytes=64) for m in range(HALVES)]
         wh8_s = [sb.tile([P, P], U8, name=f"wh8_s{m}", align_bytes=64) for m in range(HALVES)]
         gate = [sb.tile([P, J], F32, name=f"gate{m}") for m in range(HALVES)]
         made = [sb.tile([P, J], F32, name=f"made{m}") for m in range(HALVES)]
@@ -124,8 +114,8 @@ def tile_list_hwayt_qf_tanh_kernel(
         def gather_words(a, js):
             nc.vector.tensor_copy(got_w[a][:, js], tab_w[a][:].indirect(picks(js)))
 
-        def round_wh8(m, copy):
-            copy(
+        def round_wh8(m):
+            nc.scalar.copy(
                 grouped[m][:].rearrange("p (c e) i -> p c i e", e=4),
                 wh8_raw[:, :, cols[m]].rearrange("p i (c e) -> p c i e", e=4),
             )
@@ -138,11 +128,8 @@ def tile_list_hwayt_qf_tanh_kernel(
         def table(a, js):
             return dict(rhs=got_w[a][:, js].bitcast(FP8X4), rhs_scale=scales[FIRST[a] : P, js])
 
-        def within(js, part):
-            return slice(part.start - js.start, part.stop - js.start)
-
-        def make_gate(m, js, parts):
-            tag = "ha0_0" if (m, js) == (1, RIGHT) else f"ga{m}_{js.start}"
+        def make_gate(m, js):
+            tag = "ha0_0" if (m, js) == (HALVES - 1, RIGHT) else f"ga{m}_{js.start}"
             acc = ps.tile([P, js.stop - js.start], F32, name=f"ga{m}_{js.start}", tag=tag)
             for a in range(PASSES):
                 nc.tensor.matmul_mx(
@@ -153,8 +140,7 @@ def tile_list_hwayt_qf_tanh_kernel(
                     stop=(a == PASSES - 1),
                     **table(a, js),
                 )
-            for part in parts:
-                nc.scalar.activation(gate[m][:, part], acc[:, within(js, part)], ACT.Tanh, bias=half_bias[:, m : m + 1], scale=0.5)
+            nc.scalar.activation(gate[m][:, js], acc[:], ACT.Tanh, bias=half_bias[:, m : m + 1], scale=0.5)
 
         def make_new(m, js):
             acc = ps.tile([P, js.stop - js.start], F32, name=f"ha{m}_{js.start}", tag=f"ha{m}_{js.start}")
@@ -185,13 +171,11 @@ def tile_list_hwayt_qf_tanh_kernel(
 
         def finish(m, js):
             nc.vector.scalar_tensor_tensor(result[m][:, js], gate[m][:, js], -0.5, made[m][:, js], ALU.mult, ALU.add)
-
-        def store(m, js, engine):
-            engine.dma_start(out[cols[m], js], result[m][:, js])
+            nc.sync.dma_start(out[cols[m], js], result[m][:, js])
 
         gather_words(0, WHOLE)
-        round_wh8(0, nc.scalar.copy)
-        round_wh8(1, nc.scalar.copy)
+        for m in range(HALVES):
+            round_wh8(m)
         quantise_wh8(0)
         got_w.append(sb.tile([P, J], U32, name="got_w1", tag="grouped0", align_bytes=64))
         for js in (EARLY, NEXT, RIGHT):
@@ -203,15 +187,11 @@ def tile_list_hwayt_qf_tanh_kernel(
             make_new(m, js)
         nc.scalar.mul(half_bias[:], bias[:], 0.5)
         for m, js in quarters:
-            make_gate(m, js, [js])
+            make_gate(m, js)
         for m, js in pieces:
             differ(m, js)
-        weigh(0, WHOLE)
-        weigh(1, LEFT)
-        finish(0, WHOLE)
-        store(0, WHOLE, nc.sync)
-        weigh(1, RIGHT)
-        finish(1, LEFT)
-        store(1, LEFT, nc.sync)
-        finish(1, RIGHT)
-        store(1, RIGHT, nc.sync)
+        weigh(*quarters[0])
+        for before, quarter in zip(quarters, quarters[1:]):
+            weigh(*quarter)
+            finish(*before)
+        finish(*quarters[-1])

@@ -91,8 +91,8 @@ def tile_list_hwayt_qf_tanh_kernel(
                 rows[q : PASSES * BLOCKS : QUADS, :],
             )
         nc.sync.dma_start(carry[0][:], rT[cols[0], :])
-        load_wg(0)
         nc.sync.dma_start(carry[1][:], rT[cols[1], :])
+        load_wg(0)
         with nc.allow_non_contiguous_dma(reason="one bias value for each partition and half"):
             nc.sync.dma_start(bias[:], bg.rearrange("(m p) -> p m", p=P))
         load_wg(1)
@@ -152,15 +152,14 @@ def tile_list_hwayt_qf_tanh_kernel(
                 stop=False,
                 **table(0, js),
             )
-            for j0 in range(js.start, js.stop, P):
-                nc.tensor.matmul_mx(
-                    out=acc[:, j0 - js.start : j0 - js.start + P],
-                    lhsT=wh4_w[:, 2 * m * P : 2 * (m + 1) * P].bitcast(FP4X4),
-                    lhsT_scale=scales[:, WH4_AT + m * P : WH4_AT + (m + 1) * P],
-                    start=False,
-                    stop=(j0 + P == js.stop),
-                    **table(1, slice(j0, j0 + P)),
-                )
+            nc.tensor.matmul_mx(
+                out=acc[:],
+                lhsT=wh4_w[:, 2 * m * P : 2 * (m + 1) * P].bitcast(FP4X4),
+                lhsT_scale=scales[:, WH4_AT + m * P : WH4_AT + (m + 1) * P],
+                start=False,
+                stop=True,
+                **table(1, js),
+            )
             nc.scalar.activation(made[m][:, js], acc[:], ACT.Tanh)
 
         def differ(m, js):

@@ -26,6 +26,7 @@ HALVES = N // P
 GROUP = 16
 LEFT, RIGHT, WHOLE = slice(0, J // 2), slice(J // 2, J), slice(0, J)
 EARLY, NEXT = slice(0, P), slice(P, 2 * P)
+LAST = (slice(2 * P, 3 * P), slice(3 * P, J))
 FIRST = (4, 0)
 WG_AT, WH4_AT, SCALE_COLS = J, J + N, J + 2 * N
 
@@ -63,8 +64,8 @@ def tile_list_hwayt_qf_tanh_kernel(
                 tile[first : first + BLOCKS, :], source.bitcast(I32).rearrange("(q r) t -> r q t", q=QUADS)
             )
 
-        def load_words(a):
-            nc.sync.dma_start(tab_w[a][:].bitcast(I32), tab_words[a].rearrange("p t i -> p (t i)").bitcast(I32))
+        def load_words(engine, a):
+            engine.dma_start(tab_w[a][:].bitcast(I32), tab_words[a].rearrange("p t i -> p (t i)").bitcast(I32))
 
         def load_wg(m):
             nc.sync.dma_start(
@@ -74,12 +75,12 @@ def tile_list_hwayt_qf_tanh_kernel(
         nc.sync.dma_start(offsets[:], offs)
         load_rows(nc.scalar, tab_s[:].bitcast(I32), tab_scales[1], 1)
         load_rows(nc.sync, tab_s[:].bitcast(I32), tab_scales[0], 0)
-        for a in range(PASSES):
-            load_rows(nc.scalar, rows[:, WG_AT // PACK : WH4_AT // PACK], wg_scales[a], a)
-        load_words(0)
+        load_words(nc.scalar, 0)
+        for a, engine in enumerate((nc.scalar, nc.sync)):
+            load_rows(engine, rows[:, WG_AT // PACK : WH4_AT // PACK], wg_scales[a], a)
         load_rows(nc.sync, rows[:, WH4_AT // PACK :], wh4_scales[0], 1)
         nc.sync.dma_start(wh8_raw[:], wh8.rearrange("(p i) n -> p i n", i=PACK))
-        load_words(1)
+        load_words(nc.sync, 1)
         nc.sync.dma_start(wh4_w[:].bitcast(I32), wh4_words[0].bitcast(I32))
 
         got_s = sb.tile([P, J], U8, name="got_s", align_bytes=64)
@@ -91,10 +92,10 @@ def tile_list_hwayt_qf_tanh_kernel(
                 rows[q : PASSES * BLOCKS : QUADS, :],
             )
         nc.sync.dma_start(carry[0][:], rT[cols[0], :])
-        nc.sync.dma_start(carry[1][:], rT[cols[1], :])
-        load_wg(0)
         with nc.allow_non_contiguous_dma(reason="one bias value for each partition and half"):
             nc.sync.dma_start(bias[:], bg.rearrange("(m p) -> p m", p=P))
+        nc.sync.dma_start(carry[1][:], rT[cols[1], :])
+        load_wg(0)
         load_wg(1)
 
         def picks(js):
@@ -193,4 +194,5 @@ def tile_list_hwayt_qf_tanh_kernel(
         for before, quarter in zip(quarters, quarters[1:]):
             weigh(*quarter)
             finish(*before)
-        finish(*quarters[-1])
+        for js in LAST:
+            finish(HALVES - 1, js)

@@ -92,10 +92,10 @@ def tile_list_hwayt_qf_tanh_kernel(
                 rows[q : PASSES * BLOCKS : QUADS, :],
             )
         nc.sync.dma_start(carry[0][:], rT[cols[0], :])
-        with nc.allow_non_contiguous_dma(reason="one bias value for each partition and half"):
-            nc.sync.dma_start(bias[:], bg.rearrange("(m p) -> p m", p=P))
         nc.sync.dma_start(carry[1][:], rT[cols[1], :])
         load_wg(0)
+        with nc.allow_non_contiguous_dma(reason="one bias value for each partition and half"):
+            nc.sync.dma_start(bias[:], bg.rearrange("(m p) -> p m", p=P))
         load_wg(1)
 
         def picks(js):

@@ -112,6 +112,8 @@ def tile_list_hwayt_qf_tanh_kernel(
         diff = [sb.tile([P, J], F32, name=f"diff{m}") for m in range(HALVES)]
         result = [sb.tile([P, J], F32, name=f"result{m}") for m in range(HALVES)]
 
+        picked = sb.tile([P, J // 2], F32, name="picked")
+
         def gather_words(a, js):
             nc.vector.tensor_copy(got_w[a][:, js], tab_w[a][:].indirect(picks(js)))
 
@@ -130,7 +132,7 @@ def tile_list_hwayt_qf_tanh_kernel(
             return dict(rhs=got_w[a][:, js].bitcast(FP8X4), rhs_scale=scales[FIRST[a] : P, js])
 
         def make_gate(m, js):
-            tag = "ha0_0" if (m, js) == (HALVES - 1, RIGHT) else f"ga{m}_{js.start}"
+            tag = f"ga{m}_{js.start}"
             acc = ps.tile([P, js.stop - js.start], F32, name=f"ga{m}_{js.start}", tag=tag)
             for a in range(PASSES):
                 nc.tensor.matmul_mx(
@@ -166,6 +168,9 @@ def tile_list_hwayt_qf_tanh_kernel(
         def differ(m, js):
             nc.vector.tensor_tensor(diff[m][:, js], carry[m][:].indirect(picks(js)), made[m][:, js], ALU.subtract)
 
+        def subtract(js):
+            nc.vector.tensor_tensor(diff[0][:, js], picked[:], made[0][:, js], ALU.subtract)
+
         def weigh(m, js):
             nc.vector.scalar_tensor_tensor(gate[m][:, js], gate[m][:, js], -1.0, diff[m][:, js], ALU.add, ALU.mult)
 
@@ -178,18 +183,21 @@ def tile_list_hwayt_qf_tanh_kernel(
             round_wh8(m)
         quantise_wh8(0)
         got_w.append(sb.tile([P, J], U32, name="got_w1", tag="grouped0", align_bytes=64))
-        for js in (EARLY, NEXT, RIGHT):
+        for js in (LEFT, RIGHT):
             gather_words(1, js)
         quantise_wh8(1)
         quarters = [(m, js) for m in range(HALVES) for js in (LEFT, RIGHT)]
-        pieces = [(0, EARLY), (0, NEXT)] + quarters[1:]
+        pieces = quarters
+        nc.vector.tensor_copy(picked[:], carry[0][:].indirect(picks(RIGHT)))
         for m, js in pieces:
             make_new(m, js)
         nc.scalar.mul(half_bias[:], bias[:], 0.5)
         for m, js in quarters:
             make_gate(m, js)
-        for m, js in pieces:
-            differ(m, js)
+        differ(0, LEFT)
+        subtract(RIGHT)
+        differ(1, LEFT)
+        differ(1, RIGHT)
         weigh(*quarters[0])
         for before, quarter in zip(quarters, quarters[1:]):
             weigh(*quarter)

@@ -25,10 +25,8 @@ BLOCKS = 16
 HALVES = N // P
 GROUP = 16
 LEFT, RIGHT, WHOLE = slice(0, J // 2), slice(J // 2, J), slice(0, J)
-EARLY, NEXT = slice(0, P), slice(P, 2 * P)
 LAST = (slice(2 * P, 3 * P), slice(3 * P, J))
-FIRST = (4, 0)
-WG_AT, WH4_AT, SCALE_COLS = J, J + N, J + 2 * N
+WG_AT, WH4_AT, SCALE_COLS = J, J + N, J + N + P
 
 
 def tile_list_hwayt_qf_tanh_kernel(
@@ -51,18 +49,14 @@ def tile_list_hwayt_qf_tanh_kernel(
         bias = sb.tile([P, HALVES], F32, name="bias")
         half_bias = sb.tile([P, HALVES], F32, name="half_bias")
         rows = sb.tile([PASSES * BLOCKS, SCALE_COLS // PACK], I32, name="rows", align_bytes=64)
-        scales = sb.tile([P, SCALE_COLS], U8, name="scales", align_bytes=64)
+        scales = sb.tile([P, PASSES * SCALE_COLS], U8, name="scales", align_bytes=64)
 
-        nc.vector.memset(rows[:, WH4_AT // PACK :], 0)
         nc.vector.memset(tab_s[:].bitcast(I32)[QUAD : 2 * QUAD, :], 0)
         nc.vector.memset(tab_s[:].bitcast(I32)[2 * QUAD : P, :], 0)
         nc.vector.memset(scales[:].bitcast(I32), 0)
 
-        def load_rows(engine, tile, source, a):
-            first = BLOCKS * (1 - a)
-            engine.dma_start(
-                tile[first : first + BLOCKS, :], source.bitcast(I32).rearrange("(q r) t -> r q t", q=QUADS)
-            )
+        def load_rows(engine, tile, source):
+            engine.dma_start(tile, source.bitcast(I32).rearrange("a (q r) t -> r (a q) t", q=QUADS))
 
         def load_words(engine, a):
             engine.dma_start(tab_w[a][:].bitcast(I32), tab_words[a].rearrange("p t i -> p (t i)").bitcast(I32))
@@ -73,12 +67,13 @@ def tile_list_hwayt_qf_tanh_kernel(
             )
 
         nc.sync.dma_start(offsets[:], offs)
-        load_rows(nc.scalar, tab_s[:].bitcast(I32), tab_scales[1], 1)
-        load_rows(nc.sync, tab_s[:].bitcast(I32), tab_scales[0], 0)
+        load_rows(nc.scalar, tab_s[:].bitcast(I32)[0:QUAD, :], tab_scales)
         load_words(nc.scalar, 0)
-        for a, engine in enumerate((nc.scalar, nc.sync)):
-            load_rows(engine, rows[:, WG_AT // PACK : WH4_AT // PACK], wg_scales[a], a)
-        load_rows(nc.sync, rows[:, WH4_AT // PACK :], wh4_scales[0], 1)
+        load_rows(nc.sync, rows[:, WG_AT // PACK : WH4_AT // PACK], wg_scales)
+        nc.sync.dma_start(
+            rows[:, WH4_AT // PACK :],
+            wh4_scales[0].bitcast(I32).rearrange("(q r) (m n) -> (r m) q n", q=QUADS, m=HALVES),
+        )
         nc.sync.dma_start(wh8_raw[:], wh8.rearrange("(p i) n -> p i n", i=PACK))
         load_words(nc.sync, 1)
         nc.sync.dma_start(wh4_w[:].bitcast(I32), wh4_words[0].bitcast(I32))
@@ -88,7 +83,7 @@ def tile_list_hwayt_qf_tanh_kernel(
         nc.vector.tensor_copy(rows[:, : J // PACK], got_s[:].bitcast(I32)[0 : PASSES * BLOCKS, :])
         for q in range(QUADS):
             nc.sync.dma_start(
-                scales[:].bitcast(I32)[QUAD * q : QUAD * q + PASSES * BLOCKS // QUADS, :],
+                scales[:].bitcast(I32)[QUAD * q : QUAD * q + PACK, :].rearrange("r (a c) -> r a c", a=PASSES),
                 rows[q : PASSES * BLOCKS : QUADS, :],
             )
         nc.sync.dma_start(carry[0][:], rT[cols[0], :])
@@ -128,8 +123,11 @@ def tile_list_hwayt_qf_tanh_kernel(
                 out=wh8_w[m][:].bitcast(FP8X4), scales=wh8_s[m][:], in_=grouped[m][:].rearrange("p c i -> p (c i)")
             )
 
+        def plane(a, start, stop):
+            return scales[:, a * SCALE_COLS + start : a * SCALE_COLS + stop]
+
         def table(a, js):
-            return dict(rhs=got_w[a][:, js].bitcast(FP8X4), rhs_scale=scales[FIRST[a] : P, js])
+            return dict(rhs=got_w[a][:, js].bitcast(FP8X4), rhs_scale=plane(a, js.start, js.stop))
 
         def make_gate(m, js):
             tag = f"ga{m}_{js.start}"
@@ -138,7 +136,7 @@ def tile_list_hwayt_qf_tanh_kernel(
                 nc.tensor.matmul_mx(
                     out=acc[:],
                     lhsT=wg_w[m][:, a, :].bitcast(FP8X4),
-                    lhsT_scale=scales[FIRST[a] : P, WG_AT + m * P : WG_AT + (m + 1) * P],
+                    lhsT_scale=plane(a, WG_AT + m * P, WG_AT + (m + 1) * P),
                     start=(a == 0),
                     stop=(a == PASSES - 1),
                     **table(a, js),
@@ -158,7 +156,7 @@ def tile_list_hwayt_qf_tanh_kernel(
             nc.tensor.matmul_mx(
                 out=acc[:],
                 lhsT=wh4_w[:, 2 * m * P : 2 * (m + 1) * P].bitcast(FP4X4),
-                lhsT_scale=scales[:, WH4_AT + m * P : WH4_AT + (m + 1) * P],
+                lhsT_scale=plane(m, WH4_AT, SCALE_COLS),
                 start=False,
                 stop=True,
                 **table(1, js),

@@ -56,7 +56,7 @@ def tile_list_hwayt_qf_tanh_kernel(
         nc.vector.memset(scales[:].bitcast(I32), 0)
 
         def load_rows(engine, tile, source):
-            engine.dma_start(tile, source.bitcast(I32).rearrange("a (q r) t -> r (a q) t", q=QUADS))
+            engine.dma_start(tile, source.bitcast(I32).rearrange("a b t -> b a t"))
 
         def load_words(engine, a):
             engine.dma_start(tab_w[a][:].bitcast(I32), tab_words[a].rearrange("p t i -> p (t i)").bitcast(I32))
@@ -72,7 +72,7 @@ def tile_list_hwayt_qf_tanh_kernel(
         load_rows(nc.sync, rows[:, WG_AT // PACK : WH4_AT // PACK], wg_scales)
         nc.sync.dma_start(
             rows[:, WH4_AT // PACK :],
-            wh4_scales[0].bitcast(I32).rearrange("(q r) (m n) -> (r m) q n", q=QUADS, m=HALVES),
+            wh4_scales[0].bitcast(I32).rearrange("b (m n) -> (b m) n", m=HALVES),
         )
         nc.sync.dma_start(wh8_raw[:], wh8.rearrange("(p i) n -> p i n", i=PACK))
         load_words(nc.sync, 1)
@@ -81,10 +81,10 @@ def tile_list_hwayt_qf_tanh_kernel(
         got_s = sb.tile([P, J], U8, name="got_s", align_bytes=64)
         nc.vector.tensor_copy(got_s[:], tab_s[:].indirect(offsets[:]))
         nc.vector.tensor_copy(rows[:, : J // PACK], got_s[:].bitcast(I32)[0 : PASSES * BLOCKS, :])
-        for q in range(QUADS):
+        for q in (0, 2, 1, 3):
             nc.sync.dma_start(
                 scales[:].bitcast(I32)[QUAD * q : QUAD * q + PACK, :].rearrange("r (a c) -> r a c", a=PASSES),
-                rows[q : PASSES * BLOCKS : QUADS, :],
+                rows[PASSES * PACK * q : PASSES * PACK * (q + 1), :],
             )
         nc.sync.dma_start(carry[0][:], rT[cols[0], :])
         nc.sync.dma_start(carry[1][:], rT[cols[1], :])

from contextlib import ExitStack

import concourse.mybir as mybir

K, N, T, J = 1024, 256, 1024, 512
FLOPS = 2 * 2 * K * N * J

F32 = mybir.dt.float32
BF16 = mybir.dt.bfloat16
I32 = mybir.dt.int32
U32 = mybir.dt.uint32
U16 = mybir.dt.uint16
U8 = mybir.dt.uint8
FP8X4 = mybir.dt.float8_e4m3fn_x4
FP4X4 = mybir.dt.float4_e2m1fn_x4
ACT = mybir.ActivationFunctionType
ALU = mybir.AluOpType

P = 128
PACK = 4
QUADS = 4
QUAD = P // QUADS
PASSES = 2
BLOCKS = 16
HALVES = N // P
GROUP = 16
LEFT, RIGHT, WHOLE = slice(0, J // 2), slice(J // 2, J), slice(0, J)
LAST = (slice(2 * P, 3 * P), slice(3 * P, J))
WG_AT, WH4_AT, SCALE_COLS = J, J + N, J + N + P


def tile_list_hwayt_qf_tanh_kernel(
    tc, tab_words, tab_scales, wg_words, wg_scales, wh8, wh4_words, wh4_scales, bg, rT, offs, out
):
    nc = tc.nc
    with ExitStack() as ctx:
        sb = ctx.enter_context(tc.tile_pool(name="sb", bufs=1))
        ps = ctx.enter_context(tc.psum_pool(name="ps", bufs=1))
        held = ctx.enter_context(tc.tile_pool(name="held", bufs=1))

        cols = [slice(m * P, (m + 1) * P) for m in range(HALVES)]
        offsets = held.tile([P, J // GROUP], U16, name="offsets")
        tab_w = [sb.tile([P, T], U32, name=f"tab_w{a}", align_bytes=64) for a in range(PASSES)]
        tab_s = sb.tile([P, T], U8, name="tab_s", align_bytes=64)
        wg_w = [sb.tile([P, PASSES, P], U32, name=f"wg_w{m}", align_bytes=64) for m in range(HALVES)]
        wh4_w = sb.tile([P, 2 * N], U8, name="wh4_w", align_bytes=64)
        wh8_raw = sb.tile([P, PACK, N], F32, name="wh8_raw", align_bytes=64)
        carry = [sb.tile([P, T], F32, name=f"carry{m}", align_bytes=64) for m in range(HALVES)]
        bias = sb.tile([P, HALVES], F32, name="bias")
        half_bias = sb.tile([P, HALVES], F32, name="half_bias")
        rows = sb.tile([PASSES * BLOCKS, SCALE_COLS // PACK], I32, name="rows", align_bytes=64)
        scales = sb.tile([P, PASSES * SCALE_COLS], U8, name="scales", align_bytes=64)

        nc.vector.memset(tab_s[:].bitcast(I32)[QUAD : 2 * QUAD, :], 0)
        nc.vector.memset(tab_s[:].bitcast(I32)[2 * QUAD : P, :], 0)
        nc.vector.memset(scales[:].bitcast(I32), 0)

        def load_rows(engine, tile, source):
            engine.dma_start(tile, source.bitcast(I32).rearrange("a b t -> b a t"))

        def load_words(engine, a):
            engine.dma_start(tab_w[a][:].bitcast(I32), tab_words[a].rearrange("p t i -> p (t i)").bitcast(I32))

        def load_wg(m):
            nc.sync.dma_start(
                wg_w[m][:].bitcast(I32), wg_words[:, :, cols[m], :].rearrange("a p n i -> p a (n i)").bitcast(I32)
            )

        nc.sync.dma_start(offsets[:], offs)
        load_rows(nc.scalar, tab_s[:].bitcast(I32)[0:QUAD, :], tab_scales)
        load_words(nc.scalar, 0)
        load_rows(nc.sync, rows[:, WG_AT // PACK : WH4_AT // PACK], wg_scales)
        nc.sync.dma_start(
            rows[:, WH4_AT // PACK :],
            wh4_scales[0].bitcast(I32).rearrange("b (m n) -> (b m) n", m=HALVES),
        )
        nc.sync.dma_start(wh8_raw[:], wh8.rearrange("(p i) n -> p i n", i=PACK))
        load_words(nc.sync, 1)
        nc.sync.dma_start(wh4_w[:].bitcast(I32), wh4_words[0].bitcast(I32))

        got_s = sb.tile([P, J], U8, name="got_s", align_bytes=64)
        nc.vector.tensor_copy(got_s[:], tab_s[:].indirect(offsets[:]))
        nc.vector.tensor_copy(rows[:, : J // PACK], got_s[:].bitcast(I32)[0 : PASSES * BLOCKS, :])
        for q in (0, 2, 1, 3):
            nc.sync.dma_start(
                scales[:].bitcast(I32)[QUAD * q : QUAD * q + PACK, :].rearrange("r (a c) -> r a c", a=PASSES),
                rows[PASSES * PACK * q : PASSES * PACK * (q + 1), :],
            )
        nc.sync.dma_start(carry[0][:], rT[cols[0], :])
        nc.sync.dma_start(carry[1][:], rT[cols[1], :])
        load_wg(0)
        with nc.allow_non_contiguous_dma(reason="one bias value for each partition and half"):
            nc.sync.dma_start(bias[:], bg.rearrange("(m p) -> p m", p=P))
        load_wg(1)

        def picks(js):
            return offsets[:, js.start // GROUP : js.stop // GROUP]

        grouped = [
            sb.tile([P, P, PACK], BF16, name=f"grouped{m}", tag=f"grouped{m}", align_bytes=64) for m in range(HALVES)
        ]
        got_w = [sb.tile([P, J], U32, name="got_w0", align_bytes=64)]
        wh8_w = [sb.tile([P, P], U32, name=f"wh8_w{m}", align_bytes=64) for m in range(HALVES)]
        wh8_s = [sb.tile([P, P], U8, name=f"wh8_s{m}", align_bytes=64) for m in range(HALVES)]
        gate = [sb.tile([P, J], F32, name=f"gate{m}") for m in range(HALVES)]
        made = [sb.tile([P, J], F32, name=f"made{m}") for m in range(HALVES)]
        diff = [sb.tile([P, J], F32, name=f"diff{m}") for m in range(HALVES)]
        result = [sb.tile([P, J], F32, name=f"result{m}") for m in range(HALVES)]

        picked = sb.tile([P, J // 2], F32, name="picked")

        def gather_words(a, js):
            nc.vector.tensor_copy(got_w[a][:, js], tab_w[a][:].indirect(picks(js)))

        def round_wh8(m):
            nc.scalar.copy(
                grouped[m][:].rearrange("p (c e) i -> p c i e", e=4),
                wh8_raw[:, :, cols[m]].rearrange("p i (c e) -> p c i e", e=4),
            )

        def quantise_wh8(m):
            nc.vector.quantize_mx(
                out=wh8_w[m][:].bitcast(FP8X4), scales=wh8_s[m][:], in_=grouped[m][:].rearrange("p c i -> p (c i)")
            )

        def plane(a, start, stop):
            return scales[:, a * SCALE_COLS + start : a * SCALE_COLS + stop]

        def table(a, js):
            return dict(rhs=got_w[a][:, js].bitcast(FP8X4), rhs_scale=plane(a, js.start, js.stop))

        def make_gate(m, js):
            tag = f"ga{m}_{js.start}"
            acc = ps.tile([P, js.stop - js.start], F32, name=f"ga{m}_{js.start}", tag=tag)
            for a in range(PASSES):
                nc.tensor.matmul_mx(
                    out=acc[:],
                    lhsT=wg_w[m][:, a, :].bitcast(FP8X4),
                    lhsT_scale=plane(a, WG_AT + m * P, WG_AT + (m + 1) * P),
                    start=(a == 0),
                    stop=(a == PASSES - 1),
                    **table(a, js),
                )
            nc.scalar.activation(gate[m][:, js], acc[:], ACT.Tanh, bias=half_bias[:, m : m + 1], scale=0.5)

        def make_new(m, js):
            acc = ps.tile([P, js.stop - js.start], F32, name=f"ha{m}_{js.start}", tag=f"ha{m}_{js.start}")
            nc.tensor.matmul_mx(
                out=acc[:],
                lhsT=wh8_w[m][:].bitcast(FP8X4),
                lhsT_scale=wh8_s[m][:],
                start=True,
                stop=False,
                **table(0, js),
            )
            nc.tensor.matmul_mx(
                out=acc[:],
                lhsT=wh4_w[:, 2 * m * P : 2 * (m + 1) * P].bitcast(FP4X4),
                lhsT_scale=plane(m, WH4_AT, SCALE_COLS),
                start=False,
                stop=True,
                **table(1, js),
            )
            nc.scalar.activation(made[m][:, js], acc[:], ACT.Tanh)

        def differ(m, js):
            nc.vector.tensor_tensor(diff[m][:, js], carry[m][:].indirect(picks(js)), made[m][:, js], ALU.subtract)

        def subtract(js):
            nc.vector.tensor_tensor(diff[0][:, js], picked[:], made[0][:, js], ALU.subtract)

        def weigh(m, js):
            nc.vector.scalar_tensor_tensor(gate[m][:, js], gate[m][:, js], -1.0, diff[m][:, js], ALU.add, ALU.mult)

        def finish(m, js):
            nc.vector.scalar_tensor_tensor(result[m][:, js], gate[m][:, js], -0.5, made[m][:, js], ALU.mult, ALU.add)
            nc.sync.dma_start(out[cols[m], js], result[m][:, js])

        gather_words(0, WHOLE)
        for m in range(HALVES):
            round_wh8(m)
        quantise_wh8(0)
        got_w.append(sb.tile([P, J], U32, name="got_w1", tag="grouped0", align_bytes=64))
        for js in (LEFT, RIGHT):
            gather_words(1, js)
        quantise_wh8(1)
        quarters = [(m, js) for m in range(HALVES) for js in (LEFT, RIGHT)]
        pieces = quarters
        nc.vector.tensor_copy(picked[:], carry[0][:].indirect(picks(RIGHT)))
        for m, js in pieces:
            make_new(m, js)
        nc.scalar.mul(half_bias[:], bias[:], 0.5)
        for m, js in quarters:
            make_gate(m, js)
        differ(0, LEFT)
        subtract(RIGHT)
        differ(1, LEFT)
        differ(1, RIGHT)
        weigh(*quarters[0])
        for before, quarter in zip(quarters, quarters[1:]):
            weigh(*quarter)
            finish(*before)
        for js in LAST:
            finish(HALVES - 1, js)
